import numpy as np
import ml_dtypes


def mxq(x, axis, fmt="e4m3"):
    dtype, down = {"e4m3": (ml_dtypes.float8_e4m3fn, 7), "e5m2": (ml_dtypes.float8_e5m2, 14)}[fmt]
    v = np.moveaxis(np.asarray(x, np.float32).astype(ml_dtypes.bfloat16).astype(np.float64), axis, -1)
    blocks = v.reshape(v.shape[:-1] + (-1, 32))
    amax = np.abs(blocks).max(-1, keepdims=True)
    byte = np.maximum(np.where(amax > 0, np.frexp(amax)[1] - 1 + 127, 0) - down, 1)
    scale = np.exp2(byte - 127.0)
    codes = (blocks / scale).astype(np.float32).astype(dtype).astype(np.float64)
    return np.moveaxis((codes * scale).reshape(v.shape), -1, axis)


WIDE = False


def mx_kscale(k):
    if not WIDE:
        return np.ones(k)
    levels = np.array([10, -10, 5, -5, 0])
    if k % 512:
        return np.exp2(np.random.permutation(np.resize(levels, k // 32))).repeat(32)
    a = np.empty((k // 512, 16))
    for p in range(k // 512):
        a[p, :8] = np.random.permutation(np.resize(levels, 8))
        for g in range(8):
            far = levels[np.abs(levels - a[p, g]) >= 10]
            a[p, g + 8] = far[np.random.randint(len(far))]
    return np.exp2(a.ravel()).repeat(32)


def f64(x):
    return np.asarray(x).astype(np.float64)


def striped(idx):
    return np.tile(np.asarray(idx).reshape(-1, 16).T, (8, 1)).astype(np.uint16)


def unstriped(offs):
    return offs[:16].T.reshape(-1).astype(np.int64)


E2M1 = np.array([0.0, 0.5, 1.0, 1.5, 2.0, 3.0, 4.0, 6.0, -0.0, -0.5, -1.0, -1.5, -2.0, -3.0, -4.0, -6.0])


def pack_weight(w, fmt):
    k, n = w.shape
    w = f64(np.asarray(w, np.float32).astype(ml_dtypes.bfloat16)).reshape(k // 32, 32, n)
    amax = np.abs(w).max(1)
    if fmt == "e4m3":
        byte = np.frexp(amax)[1] - 1 + 127 - 7
    else:
        mant, ex = np.frexp(amax / 6.0)
        byte = np.where(mant > 0.5, ex, ex - 1) + 127
    byte = np.clip(np.where(amax > 0, byte, 1), 1, 254)
    scaled = (w * np.exp2(127.0 - byte)[:, None, :]).reshape(k, n).astype(np.float32)
    by_word = np.ascontiguousarray(scaled.reshape(k // 512, 128, 4, n).transpose(0, 1, 3, 2))
    if fmt == "e4m3":
        words = by_word.astype(ml_dtypes.float8_e4m3fn).view(np.uint8)
    else:
        c = by_word.astype(ml_dtypes.float4_e2m1fn).view(np.uint8) & 0xF
        words = (c[..., 0::2] | (c[..., 1::2] << 4)).reshape(k // 512, 128, 2 * n)
    return np.ascontiguousarray(words), np.ascontiguousarray(byte.astype(np.uint8).reshape(k // 512, 16, n))


def unpack_weight(words, scales, fmt):
    g, _, n = scales.shape
    words = np.ascontiguousarray(words).reshape(g, 128, n, -1)
    if fmt == "e4m3":
        vals = words.view(ml_dtypes.float8_e4m3fn).astype(np.float64)
    else:
        nib = np.empty((g, 128, n, 4), np.uint8)
        nib[..., 0::2] = words & 0xF
        nib[..., 1::2] = words >> 4
        vals = E2M1[nib]
    vals = vals * np.repeat(np.exp2(scales.astype(np.float64) - 127.0), 8, axis=1)[..., None]
    return vals.transpose(0, 1, 3, 2).reshape(g * 512, n)


B, N, T, D, DV, NQ = 1, 2048, 4096, 1024, 128, 128
PAGE = 512


def setup_inputs():
    n = np.random.standard_normal
    pages = np.random.permutation(T // PAGE)[:B * N // PAGE]
    idx = (pages[:, None] * PAGE + np.arange(PAGE)[None, :]).reshape(-1)
    s = mx_kscale(D)[:, None]
    u = np.ones(T)
    u[idx] = mx_kscale(B * N)
    r = np.random.uniform(0.5, 2.0, T)
    k = n((D, T)) / s
    v = n((DV, T)) / (u * r)
    kp = pack_weight(k, "e2m1")
    vp = pack_weight(v.T, "e4m3")
    return {
        "qT": (n((B, D, NQ)) * s * (0.80 / np.sqrt(D))).astype(np.float32),
        "k_words": np.ascontiguousarray(kp[0].reshape(D // 1024, 2, 128, T, 2).transpose(0, 2, 3, 1, 4)).reshape(D // 1024, 128, T, 4),
        "k_scales": kp[1],
        "v_words": vp[0],
        "v_scales": vp[1],
        "vs": np.tile(u * r, (128, 1)).astype(np.float32),
        "kb": np.tile(n(T), (128, 1)).astype(np.float32),
        "og": n((B, NQ, DV)).astype(np.float32),
        "offs": striped(idx),
        "voffs": striped((pages[:, None] * DV + np.arange(DV)[None, :]).reshape(-1)),
    }


def reference(qT, k_words, k_scales, v_words, v_scales, vs, kb, og, offs, voffs):
    idx = unstriped(offs)
    k = unpack_weight(k_words.reshape(D // 1024, 128, T, 2, 2).transpose(0, 3, 1, 2, 4).reshape(D // 512, 128, 2 * T), k_scales, "e2m1")
    v = unpack_weight(v_words, v_scales, "e4m3")
    v = v.reshape(T // 512, 512, DV)[unstriped(voffs)[::DV] // DV].reshape(B, N, DV)
    pick = lambda x: x[:, idx].reshape(x.shape[0], B, N).transpose(1, 0, 2)
    q = f64(qT)
    score = mxq(q, 1, "e4m3").transpose(0, 2, 1) @ pick(k)
    score = score + pick(f64(kb))[:, :1, :]
    m = score.max(-1, keepdims=True)
    p = np.exp(score - m)
    total = p.sum(-1, keepdims=True)
    w = p * pick(f64(vs))[:, :1, :]
    y = mxq(w, 2, "e4m3") @ v
    y = y / total
    y = y / (1.0 + np.exp(-f64(og)))
    return y

@@ -1,0 +1,215 @@
+from contextlib import ExitStack
+
+import concourse.mybir as mybir
+from concourse.masks import make_identity
+
+F32 = mybir.dt.float32
+BF16 = mybir.dt.bfloat16
+I32 = mybir.dt.int32
+U32 = mybir.dt.uint32
+U16 = mybir.dt.uint16
+U8 = mybir.dt.uint8
+FP8X4 = mybir.dt.float8_e4m3fn_x4
+FP4X4 = mybir.dt.float4_e2m1fn_x4
+ALU = mybir.AluOpType
+ACT = mybir.ActivationFunctionType
+AXIS_X = mybir.AxisListType.X
+
+P = 128
+PACK = 4
+SLOTS, TOKENS, D, DV, NQ = 2048, 4096, 1024, 128, 128
+PAGE = 512
+PAGES = SLOTS // PAGE
+POOL_PAGES = TOKENS // PAGE
+D_PASSES = D // (P * PACK)
+QUADRANTS, QUADRANT = 4, 32
+SCALE_ROWS = 4
+LIST_ROWS = 16
+
+FLOPS = 2 * NQ * SLOTS * (D + DV)
+
+
+def tile_attend_pkv4_soft_kb_gate_kernel(tc, qT, k_words, k_scales, v_words, v_scales, vs, kb, og, offs, voffs, out):
+    nc = tc.nc
+    with ExitStack() as ctx:
+        keep = ctx.enter_context(tc.tile_pool(name="keep", bufs=1))
+        psum = ctx.enter_context(tc.psum_pool(name="psum", bufs=1))
+
+        def tiles(name, count, shape, dtype, pool=keep):
+            if pool is keep:
+                return [pool.tile(shape, dtype, name=name + str(i), align_bytes=64) for i in range(count)]
+            return [pool.tile(shape, dtype, name=name + str(i)) for i in range(count)]
+
+        offsets = keep.tile([P, SLOTS // LIST_ROWS], U16, name="offsets")
+        v_offsets = keep.tile([P, PAGES * DV // LIST_ROWS], U16, name="v_offsets")
+        k_pool = keep.tile([P, TOKENS], U32, name="k_pool", align_bytes=64)
+        ks_pool = keep.tile([P, TOKENS], U8, name="ks_pool", tag="ks_then_kb", align_bytes=64)
+        vs_pool = keep.tile([P, TOKENS], F32, name="vs_pool", tag="vs_then_v", align_bytes=64)
+        vsc_pool = keep.tile([P, POOL_PAGES * DV], U8, name="vsc_pool", align_bytes=64)
+        q_raw = keep.tile([P, D_PASSES, PACK, NQ], F32, name="q_raw", align_bytes=64)
+        og_sb = keep.tile([P, DV], F32, name="og_sb", align_bytes=64)
+        k_planes = keep.tile([P, D_PASSES * SLOTS], U8, name="k_planes", align_bytes=64)
+        identity = keep.tile([P, P], F32, name="identity", align_bytes=64)
+
+        scale_rows = D_PASSES * QUADRANTS * SCALE_ROWS
+        copies = P // scale_rows
+        nc.sync.dma_start(offsets[:], offs)
+        nc.sync.dma_start(
+            ks_pool[:].bitcast(I32),
+            k_scales.bitcast(I32).rearrange("o f t -> (o f) t").unsqueeze(1).to_broadcast([scale_rows, copies, TOKENS // 4]),
+        )
+        nc.sync.dma_start(k_pool[:].bitcast(I32), k_words[0].rearrange("p t b -> p (t b)").bitcast(I32))
+        nc.sync.dma_start(
+            q_raw[:].rearrange("p o j w -> p o (j w)"),
+            qT[0].rearrange("(o p j) w -> p o (j w)", o=D_PASSES, j=PACK),
+        )
+        nc.sync.dma_start(v_offsets[:], voffs)
+        nc.vector.memset(vs_pool[:], 0.0)
+        nc.scalar.dma_start(vs_pool[0:1, :], vs[0:1, :])
+        nc.vector.memset(k_planes[:].bitcast(I32), 0)
+        nc.vector.memset(vsc_pool[:].bitcast(I32), 0)
+        make_identity(nc, identity[:])
+        nc.gpsimd.dma_start(og_sb[:], og[0])
+        for quad in range(QUADRANTS):
+            nc.gpsimd.dma_start(
+                vsc_pool[QUADRANT * quad : QUADRANT * quad + SCALE_ROWS, :].bitcast(I32).rearrange("f (u e) -> f u e", u=POOL_PAGES),
+                v_scales[:, SCALE_ROWS * quad : SCALE_ROWS * (quad + 1), :].bitcast(I32).rearrange("u f e -> f u e"),
+            )
+
+        ks_rows = keep.tile([P, SLOTS], U8, name="ks_rows", align_bytes=64)
+        nc.vector.tensor_copy(ks_rows[:], ks_pool[:].indirect(offsets[:]))
+        for o in range(D_PASSES):
+            for quad in range(QUADRANTS):
+                first = copies * SCALE_ROWS * (QUADRANTS * o + quad)
+                nc.sync.dma_start(
+                    k_planes[QUADRANT * quad : QUADRANT * quad + SCALE_ROWS, o * SLOTS : (o + 1) * SLOTS].bitcast(I32),
+                    ks_rows[first : first + copies * SCALE_ROWS : copies, :].bitcast(I32),
+                )
+        kb_pool = keep.tile([P, TOKENS], F32, name="kb_pool", tag="ks_then_kb", align_bytes=64)
+        nc.sync.dma_start(kb_pool[:], kb)
+
+        vs_row = keep.tile([P, SLOTS], F32, name="vs_row", align_bytes=64)
+        vs_col = tiles("vs_col", PAGES, [P, PACK], F32)
+        nc.vector.tensor_copy(vs_row[:], vs_pool[:].indirect(offsets[:]))
+        v_pool = keep.tile([P, POOL_PAGES * DV], U32, name="v_pool", tag="vs_then_v", align_bytes=64)
+        for g in range(PAGES):
+            nc.sync.dma_start(
+                vs_col[g][:],
+                vs_row[0:1, g * PAGE : (g + 1) * PAGE].rearrange("o (p r) -> o p r", r=PACK),
+            )
+        nc.sync.dma_start(
+            v_pool[:].bitcast(I32).rearrange("p (u e) -> p u e", u=POOL_PAGES),
+            v_words.rearrange("u p e r -> p u (e r)").bitcast(I32),
+        )
+
+        gate_den = keep.tile([P, DV], F32, name="gate_den", align_bytes=64)
+        gate = keep.tile([P, DV], F32, name="gate", align_bytes=64)
+        exp_og = keep.tile([P, DV], F32, name="exp_og", align_bytes=64)
+        nc.scalar.activation(exp_og[:], og_sb[:], ACT.Exp, scale=-1.0)
+        nc.scalar.activation(gate_den[:], exp_og[:], ACT.Copy, bias=1.0)
+
+        q_grouped = keep.tile([P, D_PASSES, NQ, PACK], BF16, name="q_grouped", align_bytes=64)
+        q_codes = keep.tile([P, D_PASSES * NQ], U32, name="q_codes", align_bytes=64)
+        q_scales = keep.tile([P, D_PASSES * NQ], U8, name="q_scales", align_bytes=64)
+        nc.scalar.copy(q_grouped[:], q_raw[:].rearrange("p o j w -> p o w j"))
+
+        k_pairs = tiles("k_pairs", PAGES, [P, PAGE], U32)
+        k_parted = tiles("k_parted", PAGES, [P, D_PASSES, 2 * PAGE], U8)
+        raw_scores = tiles("raw_scores", PAGES, [P, PAGE], F32)
+        scores = tiles("scores", PAGES, [P, PAGE], F32)
+        score_banks = tiles("score_bank", PAGES, [P, PAGE], F32, psum)
+        page_max = keep.tile([P, PAGES], F32, name="page_max", align_bytes=64)
+        cols = PAGE // LIST_ROWS
+
+        for g in range(PAGES):
+            nc.vector.tensor_copy(k_pairs[g][:], k_pool[:].indirect(offsets[:, g * cols : (g + 1) * cols]))
+            if g > 0:
+                nc.vector.tensor_copy(
+                    k_parted[g - 1][:].bitcast(U16),
+                    k_pairs[g - 1][:].bitcast(U16).rearrange("p (s o) -> p o s", o=D_PASSES),
+                )
+        nc.vector.quantize_mx(
+            out=q_codes[:].bitcast(FP8X4), scales=q_scales[:], in_=q_grouped[:].rearrange("p o w j -> p (o w j)")
+        )
+        nc.vector.tensor_copy(
+            k_parted[PAGES - 1][:].bitcast(U16),
+            k_pairs[PAGES - 1][:].bitcast(U16).rearrange("p (s o) -> p o s", o=D_PASSES),
+        )
+        for g in range(PAGES):
+            for o in range(D_PASSES):
+                nc.tensor.matmul_mx(
+                    out=score_banks[g][:],
+                    lhsT=q_codes[:, o * NQ : (o + 1) * NQ].bitcast(FP8X4),
+                    lhsT_scale=q_scales[:, o * NQ : (o + 1) * NQ],
+                    rhs=k_parted[g][:, o, :].bitcast(FP4X4),
+                    rhs_scale=k_planes[:, o * SLOTS + g * PAGE : o * SLOTS + (g + 1) * PAGE],
+                    start=(o == 0),
+                    stop=(o == D_PASSES - 1),
+                )
+            nc.scalar.copy(raw_scores[g][:], score_banks[g][:])
+        for g in range(PAGES):
+            nc.vector.tensor_tensor(
+                scores[g][:], kb_pool[:].indirect(offsets[:, g * cols : (g + 1) * cols]), raw_scores[g][:], ALU.add
+            )
+            if g > 0:
+                nc.vector.tensor_reduce(page_max[:, g - 1 : g], scores[g - 1][:], AXIS_X, ALU.max)
+        nc.vector.tensor_reduce(page_max[:, PAGES - 1 : PAGES], scores[PAGES - 1][:], AXIS_X, ALU.max)
+        neg_max = keep.tile([P, 1], F32, name="neg_max", align_bytes=64)
+        nc.vector.tensor_reduce(neg_max[:], page_max[:], AXIS_X, ALU.max, negate=True)
+
+        v_codes = keep.tile([P, PAGES * DV], U32, name="v_codes", align_bytes=64)
+        v_plane = keep.tile([P, PAGES * DV], U8, name="v_plane", align_bytes=64)
+        nc.vector.tensor_copy(v_codes[:], v_pool[:].indirect(v_offsets[:]))
+        nc.vector.tensor_copy(v_plane[:], vsc_pool[:].indirect(v_offsets[:]))
+        nc.vector.reciprocal(gate[:], gate_den[:])
+
+        probs = tiles("probs", PAGES, [P, PACK, P], F32)
+        page_sum = keep.tile([P, PAGES], F32, name="page_sum", align_bytes=64)
+        turned = tiles("turned", 2, [P, PACK, NQ], F32, psum)
+        weights = tiles("weights", PAGES, [P, NQ, PACK], BF16)
+        w_codes = tiles("w_codes", PAGES, [P, NQ], U32)
+        w_scales = tiles("w_scales", PAGES, [P, NQ], U8)
+        y_bank = psum.tile([P, DV], F32, name="y_bank")
+
+        def finish(g):
+            nc.vector.quantize_mx(
+                out=w_codes[g][:].bitcast(FP8X4), scales=w_scales[g][:], in_=weights[g][:].rearrange("p q r -> p (q r)")
+            )
+            nc.tensor.matmul_mx(
+                out=y_bank[:],
+                lhsT=w_codes[g][:].bitcast(FP8X4),
+                lhsT_scale=w_scales[g][:],
+                rhs=v_codes[:, g * DV : (g + 1) * DV].bitcast(FP8X4),
+                rhs_scale=v_plane[:, g * DV : (g + 1) * DV],
+                start=(g == 0),
+                stop=(g == PAGES - 1),
+            )
+
+        for g in range(PAGES):
+            nc.scalar.activation(
+                probs[g][:].rearrange("p r s -> p s r"),
+                scores[g][:].rearrange("p (s r) -> p s r", r=PACK),
+                ACT.Exp,
+                bias=neg_max[:],
+                accum_out=page_sum[:, g : g + 1],
+            )
+            bank = turned[g % 2]
+            for r in range(PACK):
+                nc.tensor.transpose(bank[:, r, :], probs[g][:, r, :], identity[:])
+            nc.vector.tensor_tensor(
+                weights[g][:],
+                bank[:].rearrange("p r q -> p q r"),
+                vs_col[g][:].unsqueeze(1).to_broadcast([P, NQ, PACK]),
+                ALU.mult,
+            )
+            if g > 0:
+                finish(g - 1)
+        total = keep.tile([P, 1], F32, name="total", align_bytes=64)
+        inv_total = keep.tile([P, 1], F32, name="inv_total", align_bytes=64)
+        nc.vector.tensor_reduce(total[:], page_sum[:], AXIS_X, ALU.add)
+        finish(PAGES - 1)
+        nc.vector.reciprocal(inv_total[:], total[:])
+
+        result = keep.tile([P, DV], F32, name="result", align_bytes=64)
+        nc.vector.scalar_tensor_tensor(result[:], y_bank[:], inv_total[:], gate[:], ALU.mult, ALU.mult)
+        nc.sync.dma_start(out[0], result[:])

@@ -35,110 +35,115 @@ def tile_attend_pkv4_soft_kb_gate_kernel(tc, qT, k_words, k_scales, v_words, v_s
         keep = ctx.enter_context(tc.tile_pool(name="keep", bufs=1))
         psum = ctx.enter_context(tc.psum_pool(name="psum", bufs=1))
 
-        def tiles(name, count, shape, dtype, pool=keep):
-            if pool is keep:
-                return [pool.tile(shape, dtype, name=name + str(i), align_bytes=64) for i in range(count)]
-            return [pool.tile(shape, dtype, name=name + str(i)) for i in range(count)]
+        def sbuf(name, shape, dtype, tag=None):
+            return keep.tile(shape, dtype, name=name, tag=tag or name, align_bytes=64)
+
+        def bank(name, shape, tag=None):
+            return psum.tile(shape, F32, name=name, tag=tag or name)
 
         offsets = keep.tile([P, SLOTS // LIST_ROWS], U16, name="offsets")
         v_offsets = keep.tile([P, PAGES * DV // LIST_ROWS], U16, name="v_offsets")
-        k_pool = keep.tile([P, TOKENS], U32, name="k_pool", align_bytes=64)
-        ks_pool = keep.tile([P, TOKENS], U8, name="ks_pool", tag="ks_then_kb", align_bytes=64)
-        vs_pool = keep.tile([P, TOKENS], F32, name="vs_pool", tag="vs_then_v", align_bytes=64)
-        vsc_pool = keep.tile([P, POOL_PAGES * DV], U8, name="vsc_pool", align_bytes=64)
-        q_raw = keep.tile([P, D_PASSES, PACK, NQ], F32, name="q_raw", align_bytes=64)
-        og_sb = keep.tile([P, DV], F32, name="og_sb", align_bytes=64)
-        k_planes = keep.tile([P, D_PASSES * SLOTS], U8, name="k_planes", align_bytes=64)
-        identity = keep.tile([P, P], F32, name="identity", align_bytes=64)
+        cols = PAGE // LIST_ROWS
+
+        def page_offsets(g):
+            return offsets[:, g * cols : (g + 1) * cols]
 
         scale_rows = D_PASSES * QUADRANTS * SCALE_ROWS
-        copies = P // scale_rows
+        ks_pool = sbuf("ks_pool", [P, TOKENS], U8, "ks_then_kb")
+        k_pool = sbuf("k_pool", [P, TOKENS], U32)
+        q_raw = sbuf("q_raw", [P, D_PASSES, PACK, NQ], F32, "q_then_v")
         nc.sync.dma_start(offsets[:], offs)
-        nc.sync.dma_start(
-            ks_pool[:].bitcast(I32),
-            k_scales.bitcast(I32).rearrange("o f t -> (o f) t").unsqueeze(1).to_broadcast([scale_rows, copies, TOKENS // 4]),
-        )
+        nc.sync.dma_start(v_offsets[:], voffs)
+        nc.sync.dma_start(ks_pool[0:scale_rows, :].bitcast(I32), k_scales.bitcast(I32).rearrange("o f t -> (o f) t"))
         nc.sync.dma_start(k_pool[:].bitcast(I32), k_words[0].rearrange("p t b -> p (t b)").bitcast(I32))
         nc.sync.dma_start(
             q_raw[:].rearrange("p o j w -> p o (j w)"),
             qT[0].rearrange("(o p j) w -> p o (j w)", o=D_PASSES, j=PACK),
         )
-        nc.sync.dma_start(v_offsets[:], voffs)
-        nc.vector.memset(vs_pool[:], 0.0)
-        nc.scalar.dma_start(vs_pool[0:1, :], vs[0:1, :])
-        nc.vector.memset(k_planes[:].bitcast(I32), 0)
+
+        k_planes = sbuf("k_planes", [P, D_PASSES * SLOTS], U8)
+        vsc_pool = sbuf("vsc_pool", [P, POOL_PAGES * DV], U8)
+        nc.vector.memset(ks_pool[scale_rows : 2 * scale_rows, :].bitcast(I32), 0)
+        nc.vector.memset(ks_pool[2 * scale_rows :, :].bitcast(I32), 0)
         nc.vector.memset(vsc_pool[:].bitcast(I32), 0)
-        make_identity(nc, identity[:])
+        nc.vector.memset(k_planes[:].bitcast(I32), 0)
+
+        og_sb = sbuf("og_sb", [P, DV], F32)
+        identity = sbuf("identity", [P, P], F32)
         nc.gpsimd.dma_start(og_sb[:], og[0])
         for quad in range(QUADRANTS):
             nc.gpsimd.dma_start(
                 vsc_pool[QUADRANT * quad : QUADRANT * quad + SCALE_ROWS, :].bitcast(I32).rearrange("f (u e) -> f u e", u=POOL_PAGES),
                 v_scales[:, SCALE_ROWS * quad : SCALE_ROWS * (quad + 1), :].bitcast(I32).rearrange("u f e -> f u e"),
             )
+        make_identity(nc, identity[:])
 
-        ks_rows = keep.tile([P, SLOTS], U8, name="ks_rows", align_bytes=64)
+        half_tanh = sbuf("half_tanh", [P, DV], F32)
+        gate = sbuf("gate", [P, DV], F32)
+        nc.scalar.activation(half_tanh[:], og_sb[:], ACT.Tanh, scale=0.5)
+        nc.scalar.activation(gate[:], half_tanh[:], ACT.Copy, scale=0.5, bias=0.5)
+
+        ks_rows = sbuf("ks_rows", [P, SLOTS], U8)
         nc.vector.tensor_copy(ks_rows[:], ks_pool[:].indirect(offsets[:]))
+        kb_pool = sbuf("kb_pool", [P, TOKENS], F32, "ks_then_kb")
+        nc.sync.dma_start(kb_pool[:], kb)
         for o in range(D_PASSES):
             for quad in range(QUADRANTS):
-                first = copies * SCALE_ROWS * (QUADRANTS * o + quad)
-                nc.sync.dma_start(
+                first = SCALE_ROWS * (QUADRANTS * o + quad)
+                queue = nc.gpsimd if quad == 0 else nc.scalar
+                queue.dma_start(
                     k_planes[QUADRANT * quad : QUADRANT * quad + SCALE_ROWS, o * SLOTS : (o + 1) * SLOTS].bitcast(I32),
-                    ks_rows[first : first + copies * SCALE_ROWS : copies, :].bitcast(I32),
+                    ks_rows[first : first + SCALE_ROWS, :].bitcast(I32),
                 )
-        kb_pool = keep.tile([P, TOKENS], F32, name="kb_pool", tag="ks_then_kb", align_bytes=64)
-        nc.sync.dma_start(kb_pool[:], kb)
 
-        vs_row = keep.tile([P, SLOTS], F32, name="vs_row", align_bytes=64)
-        vs_col = tiles("vs_col", PAGES, [P, PACK], F32)
-        nc.vector.tensor_copy(vs_row[:], vs_pool[:].indirect(offsets[:]))
-        v_pool = keep.tile([P, POOL_PAGES * DV], U32, name="v_pool", tag="vs_then_v", align_bytes=64)
-        for g in range(PAGES):
-            nc.sync.dma_start(
-                vs_col[g][:],
-                vs_row[0:1, g * PAGE : (g + 1) * PAGE].rearrange("o (p r) -> o p r", r=PACK),
+        v_plane = sbuf("v_plane", [P, PAGES * DV], U8)
+        nc.vector.tensor_copy(v_plane[:], vsc_pool[:].indirect(v_offsets[:]))
+
+        q_grouped = sbuf("q_grouped", [P, D_PASSES, NQ, PACK], BF16, "q_then_pairs")
+        q_codes = sbuf("q_codes", [P, D_PASSES * NQ], U32)
+        q_scales = sbuf("q_scales", [P, D_PASSES * NQ], U8)
+        nc.scalar.copy(q_grouped[:], q_raw[:].rearrange("p o j w -> p o w j"))
+
+        pair_tags = ["pairs_then_vs", None, "q_then_pairs", None]
+        k_pairs = {}
+        k_parted = {}
+
+        def gather_keys(g):
+            k_pairs[g] = sbuf("k_pairs%d" % g, [P, PAGE], U32, pair_tags[g])
+            nc.vector.tensor_copy(k_pairs[g][:], k_pool[:].indirect(page_offsets(g)))
+
+        def part_keys(g):
+            k_parted[g] = sbuf("k_parted%d" % g, [P, D_PASSES, 2 * PAGE], U8)
+            nc.vector.tensor_copy(
+                k_parted[g][:].bitcast(U16),
+                k_pairs[g][:].bitcast(U16).rearrange("p (s o) -> p o s", o=D_PASSES),
             )
+
+        gather_keys(0)
+        gather_keys(1)
+        part_keys(0)
+        vs_pool = sbuf("vs_pool", [P, TOKENS], F32, "pairs_then_vs")
+        nc.sync.dma_start(vs_pool[:], vs)
+        v_pool = sbuf("v_pool", [P, POOL_PAGES * DV], U32, "q_then_v")
         nc.sync.dma_start(
             v_pool[:].bitcast(I32).rearrange("p (u e) -> p u e", u=POOL_PAGES),
             v_words.rearrange("u p e r -> p u (e r)").bitcast(I32),
         )
-
-        gate_den = keep.tile([P, DV], F32, name="gate_den", align_bytes=64)
-        gate = keep.tile([P, DV], F32, name="gate", align_bytes=64)
-        exp_og = keep.tile([P, DV], F32, name="exp_og", align_bytes=64)
-        nc.scalar.activation(exp_og[:], og_sb[:], ACT.Exp, scale=-1.0)
-        nc.scalar.activation(gate_den[:], exp_og[:], ACT.Copy, bias=1.0)
-
-        q_grouped = keep.tile([P, D_PASSES, NQ, PACK], BF16, name="q_grouped", align_bytes=64)
-        q_codes = keep.tile([P, D_PASSES * NQ], U32, name="q_codes", align_bytes=64)
-        q_scales = keep.tile([P, D_PASSES * NQ], U8, name="q_scales", align_bytes=64)
-        nc.scalar.copy(q_grouped[:], q_raw[:].rearrange("p o j w -> p o w j"))
-
-        k_pairs = tiles("k_pairs", PAGES, [P, PAGE], U32)
-        k_parted = tiles("k_parted", PAGES, [P, D_PASSES, 2 * PAGE], U8)
-        raw_scores = tiles("raw_scores", PAGES, [P, PAGE], F32)
-        scores = tiles("scores", PAGES, [P, PAGE], F32)
-        score_banks = tiles("score_bank", PAGES, [P, PAGE], F32, psum)
-        page_max = keep.tile([P, PAGES], F32, name="page_max", align_bytes=64)
-        cols = PAGE // LIST_ROWS
-
-        for g in range(PAGES):
-            nc.vector.tensor_copy(k_pairs[g][:], k_pool[:].indirect(offsets[:, g * cols : (g + 1) * cols]))
-            if g > 0:
-                nc.vector.tensor_copy(
-                    k_parted[g - 1][:].bitcast(U16),
-                    k_pairs[g - 1][:].bitcast(U16).rearrange("p (s o) -> p o s", o=D_PASSES),
-                )
+        part_keys(1)
         nc.vector.quantize_mx(
             out=q_codes[:].bitcast(FP8X4), scales=q_scales[:], in_=q_grouped[:].rearrange("p o w j -> p (o w j)")
         )
-        nc.vector.tensor_copy(
-            k_parted[PAGES - 1][:].bitcast(U16),
-            k_pairs[PAGES - 1][:].bitcast(U16).rearrange("p (s o) -> p o s", o=D_PASSES),
-        )
+        gather_keys(2)
+        gather_keys(3)
+        part_keys(2)
+        part_keys(3)
+
+        raw_scores = [sbuf("raw_scores%d" % g, [P, PAGE], F32) for g in range(PAGES)]
         for g in range(PAGES):
+            score_bank = bank("score_bank%d" % g, [P, PAGE], "bank%d" % g)
             for o in range(D_PASSES):
                 nc.tensor.matmul_mx(
-                    out=score_banks[g][:],
+                    out=score_bank[:],
                     lhsT=q_codes[:, o * NQ : (o + 1) * NQ].bitcast(FP8X4),
                     lhsT_scale=q_scales[:, o * NQ : (o + 1) * NQ],
                     rhs=k_parted[g][:, o, :].bitcast(FP4X4),
@@ -146,35 +151,76 @@ def tile_attend_pkv4_soft_kb_gate_kernel(tc, qT, k_words, k_scales, v_words, v_s
                     start=(o == 0),
                     stop=(o == D_PASSES - 1),
                 )
-            nc.scalar.copy(raw_scores[g][:], score_banks[g][:])
+            nc.scalar.copy(raw_scores[g][:], score_bank[:])
+
+        last = PAGES - 1
+        scores = [sbuf("scores%d" % g, [P, PAGE + (last if g == last else 0)], F32) for g in range(PAGES)]
+        neg_max = sbuf("neg_max", [P, 1], F32)
+
+        def add_bias(g):
+            nc.vector.tensor_tensor(scores[g][:, :PAGE], kb_pool[:].indirect(page_offsets(g)), raw_scores[g][:], ALU.add)
+
+        def page_max(g):
+            nc.vector.tensor_reduce(scores[last][:, PAGE + g : PAGE + g + 1], scores[g][:], AXIS_X, ALU.max)
+
+        add_bias(0)
+        for g in range(1, PAGES):
+            add_bias(g)
+            page_max(g - 1)
+        nc.vector.tensor_reduce(neg_max[:], scores[last][:], AXIS_X, ALU.max, negate=True)
+
+        probs = [sbuf("probs%d" % g, [P, PAGE], F32) for g in range(PAGES)]
+        page_sum = sbuf("page_sum", [P, PAGES], F32)
         for g in range(PAGES):
+            nc.scalar.activation(probs[g][:], scores[g][:, :PAGE], ACT.Exp, bias=neg_max[:], accum_out=page_sum[:, g : g + 1])
+
+        token_scale = [sbuf("token_scale%d" % g, [P, PAGE], F32) for g in range(PAGES)]
+        dealt = [sbuf("dealt%d" % g, [P, 2, P, 2], BF16) for g in range(PAGES)]
+        weights = [sbuf("weights%d" % g, [P, NQ, PACK], BF16) for g in range(PAGES)]
+        w_codes = [sbuf("w_codes%d" % g, [P, NQ], U32) for g in range(PAGES)]
+        w_scales = [sbuf("w_scales%d" % g, [P, NQ], U8) for g in range(PAGES)]
+        v_codes = sbuf("v_codes", [P, PAGES * DV], U32)
+        y_bank = bank("y_bank", [P, DV])
+
+        def gather_scale(g):
+            nc.vector.tensor_copy(token_scale[g][:], vs_pool[:].indirect(page_offsets(g)))
+
+        def weigh(g):
             nc.vector.tensor_tensor(
-                scores[g][:], kb_pool[:].indirect(offsets[:, g * cols : (g + 1) * cols]), raw_scores[g][:], ALU.add
+                dealt[g][:],
+                probs[g][:].rearrange("p (s u e) -> p u s e", u=2, e=2),
+                token_scale[g][:].rearrange("p (s u e) -> p u s e", u=2, e=2),
+                ALU.mult,
             )
-            if g > 0:
-                nc.vector.tensor_reduce(page_max[:, g - 1 : g], scores[g - 1][:], AXIS_X, ALU.max)
-        nc.vector.tensor_reduce(page_max[:, PAGES - 1 : PAGES], scores[PAGES - 1][:], AXIS_X, ALU.max)
-        neg_max = keep.tile([P, 1], F32, name="neg_max", align_bytes=64)
-        nc.vector.tensor_reduce(neg_max[:], page_max[:], AXIS_X, ALU.max, negate=True)
+            turned = bank("turned%d" % g, [P, 2, NQ], "bank%d" % g)
+            words = dealt[g][:].rearrange("p u s e -> p (u s e)").bitcast(F32)
+            for u in range(2):
+                nc.tensor.transpose(turned[:, u, :], words[:, u * P : (u + 1) * P], identity[:])
+            nc.scalar.copy(
+                weights[g][:].rearrange("p q r -> p (q r)").bitcast(F32).rearrange("p (q u) -> p q u", u=2),
+                turned[:].rearrange("p u q -> p q u"),
+            )
 
-        v_codes = keep.tile([P, PAGES * DV], U32, name="v_codes", align_bytes=64)
-        v_plane = keep.tile([P, PAGES * DV], U8, name="v_plane", align_bytes=64)
-        nc.vector.tensor_copy(v_codes[:], v_pool[:].indirect(v_offsets[:]))
-        nc.vector.tensor_copy(v_plane[:], vsc_pool[:].indirect(v_offsets[:]))
-        nc.vector.reciprocal(gate[:], gate_den[:])
-
-        probs = tiles("probs", PAGES, [P, PACK, P], F32)
-        page_sum = keep.tile([P, PAGES], F32, name="page_sum", align_bytes=64)
-        turned = tiles("turned", 2, [P, PACK, NQ], F32, psum)
-        weights = tiles("weights", PAGES, [P, NQ, PACK], BF16)
-        w_codes = tiles("w_codes", PAGES, [P, NQ], U32)
-        w_scales = tiles("w_scales", PAGES, [P, NQ], U8)
-        y_bank = psum.tile([P, DV], F32, name="y_bank")
-
-        def finish(g):
+        def quantise(g):
             nc.vector.quantize_mx(
                 out=w_codes[g][:].bitcast(FP8X4), scales=w_scales[g][:], in_=weights[g][:].rearrange("p q r -> p (q r)")
             )
+
+        gather_scale(0)
+        for g in range(1, PAGES):
+            gather_scale(g)
+            weigh(g - 1)
+        weigh(last)
+        total = sbuf("total", [P, 1], F32)
+        inv_total = sbuf("inv_total", [P, 1], F32)
+        nc.vector.tensor_reduce(total[:], page_sum[:], AXIS_X, ALU.add)
+        quantise(0)
+        quantise(1)
+        nc.vector.reciprocal(inv_total[:], total[:])
+        nc.vector.tensor_copy(v_codes[:], v_pool[:].indirect(v_offsets[:]))
+        quantise(2)
+        quantise(3)
+        for g in range(PAGES):
             nc.tensor.matmul_mx(
                 out=y_bank[:],
                 lhsT=w_codes[g][:].bitcast(FP8X4),
@@ -182,34 +228,9 @@ def tile_attend_pkv4_soft_kb_gate_kernel(tc, qT, k_words, k_scales, v_words, v_s
                 rhs=v_codes[:, g * DV : (g + 1) * DV].bitcast(FP8X4),
                 rhs_scale=v_plane[:, g * DV : (g + 1) * DV],
                 start=(g == 0),
-                stop=(g == PAGES - 1),
+                stop=(g == last),
             )
 
-        for g in range(PAGES):
-            nc.scalar.activation(
-                probs[g][:].rearrange("p r s -> p s r"),
-                scores[g][:].rearrange("p (s r) -> p s r", r=PACK),
-                ACT.Exp,
-                bias=neg_max[:],
-                accum_out=page_sum[:, g : g + 1],
-            )
-            bank = turned[g % 2]
-            for r in range(PACK):
-                nc.tensor.transpose(bank[:, r, :], probs[g][:, r, :], identity[:])
-            nc.vector.tensor_tensor(
-                weights[g][:],
-                bank[:].rearrange("p r q -> p q r"),
-                vs_col[g][:].unsqueeze(1).to_broadcast([P, NQ, PACK]),
-                ALU.mult,
-            )
-            if g > 0:
-                finish(g - 1)
-        total = keep.tile([P, 1], F32, name="total", align_bytes=64)
-        inv_total = keep.tile([P, 1], F32, name="inv_total", align_bytes=64)
-        nc.vector.tensor_reduce(total[:], page_sum[:], AXIS_X, ALU.add)
-        finish(PAGES - 1)
-        nc.vector.reciprocal(inv_total[:], total[:])
-
-        result = keep.tile([P, DV], F32, name="result", align_bytes=64)
+        result = sbuf("result", [P, DV], F32)
         nc.vector.scalar_tensor_tensor(result[:], y_bank[:], inv_total[:], gate[:], ALU.mult, ALU.mult)
         nc.sync.dma_start(out[0], result[:])

@@ -49,71 +49,56 @@ def tile_attend_pkv4_soft_kb_gate_kernel(tc, qT, k_words, k_scales, v_words, v_s
             return offsets[:, g * cols : (g + 1) * cols]
 
         scale_rows = D_PASSES * QUADRANTS * SCALE_ROWS
-        ks_pool = sbuf("ks_pool", [P, TOKENS], U8, "ks_then_kb")
+        ks_pool = sbuf("ks_pool", [P, TOKENS], U8, "ks_then_identity")
         k_pool = sbuf("k_pool", [P, TOKENS], U32)
-        q_raw = sbuf("q_raw", [P, D_PASSES, PACK, NQ], F32, "q_then_v")
-        nc.sync.dma_start(offsets[:], offs)
-        nc.sync.dma_start(v_offsets[:], voffs)
+        q_raw = sbuf("q_raw", [P, D_PASSES, PACK, NQ], F32)
         nc.sync.dma_start(ks_pool[0:scale_rows, :].bitcast(I32), k_scales.bitcast(I32).rearrange("o f t -> (o f) t"))
-        nc.sync.dma_start(k_pool[:].bitcast(I32), k_words[0].rearrange("p t b -> p (t b)").bitcast(I32))
+        nc.sync.dma_start(offsets[:], offs)
         nc.sync.dma_start(
             q_raw[:].rearrange("p o j w -> p o (j w)"),
             qT[0].rearrange("(o p j) w -> p o (j w)", o=D_PASSES, j=PACK),
         )
+        nc.sync.dma_start(k_pool[:].bitcast(I32), k_words[0].rearrange("p t b -> p (t b)").bitcast(I32))
+        nc.sync.dma_start(v_offsets[:], voffs)
+        kb_pool = sbuf("kb_pool", [P, TOKENS], F32)
+        nc.sync.dma_start(kb_pool[:], kb)
 
         k_planes = sbuf("k_planes", [P, D_PASSES * SLOTS], U8)
-        vsc_pool = sbuf("vsc_pool", [P, POOL_PAGES * DV], U8)
         nc.vector.memset(ks_pool[scale_rows : 2 * scale_rows, :].bitcast(I32), 0)
         nc.vector.memset(ks_pool[2 * scale_rows :, :].bitcast(I32), 0)
-        nc.vector.memset(vsc_pool[:].bitcast(I32), 0)
         nc.vector.memset(k_planes[:].bitcast(I32), 0)
 
-        og_sb = sbuf("og_sb", [P, DV], F32)
-        identity = sbuf("identity", [P, P], F32)
-        nc.gpsimd.dma_start(og_sb[:], og[0])
-        for quad in range(QUADRANTS):
-            nc.gpsimd.dma_start(
-                vsc_pool[QUADRANT * quad : QUADRANT * quad + SCALE_ROWS, :].bitcast(I32).rearrange("f (u e) -> f u e", u=POOL_PAGES),
-                v_scales[:, SCALE_ROWS * quad : SCALE_ROWS * (quad + 1), :].bitcast(I32).rearrange("u f e -> f u e"),
-            )
-        make_identity(nc, identity[:])
-
-        half_tanh = sbuf("half_tanh", [P, DV], F32)
-        gate = sbuf("gate", [P, DV], F32)
-        nc.scalar.activation(half_tanh[:], og_sb[:], ACT.Tanh, scale=0.5)
-        nc.scalar.activation(gate[:], half_tanh[:], ACT.Copy, scale=0.5, bias=0.5)
+        q_grouped = sbuf("q_grouped", [P, D_PASSES, NQ, PACK], BF16)
+        q_codes = sbuf("q_codes", [P, D_PASSES * NQ], U32)
+        q_scales = sbuf("q_scales", [P, D_PASSES * NQ], U8)
+        nc.scalar.copy(q_grouped[:], q_raw[:].rearrange("p o j w -> p o w j"))
 
         ks_rows = sbuf("ks_rows", [P, SLOTS], U8)
         nc.vector.tensor_copy(ks_rows[:], ks_pool[:].indirect(offsets[:]))
-        kb_pool = sbuf("kb_pool", [P, TOKENS], F32, "ks_then_kb")
-        nc.sync.dma_start(kb_pool[:], kb)
         for o in range(D_PASSES):
             for quad in range(QUADRANTS):
                 first = SCALE_ROWS * (QUADRANTS * o + quad)
-                queue = nc.gpsimd if quad == 0 else nc.scalar
+                queue = nc.gpsimd if first == 0 else nc.scalar
                 queue.dma_start(
                     k_planes[QUADRANT * quad : QUADRANT * quad + SCALE_ROWS, o * SLOTS : (o + 1) * SLOTS].bitcast(I32),
                     ks_rows[first : first + SCALE_ROWS, :].bitcast(I32),
                 )
 
-        v_plane = sbuf("v_plane", [P, PAGES * DV], U8)
-        nc.vector.tensor_copy(v_plane[:], vsc_pool[:].indirect(v_offsets[:]))
+        identity = sbuf("identity", [P, P], F32, "ks_then_identity")
+        make_identity(nc, identity[:])
+        nc.vector.quantize_mx(
+            out=q_codes[:].bitcast(FP8X4), scales=q_scales[:], in_=q_grouped[:].rearrange("p o w j -> p (o w j)")
+        )
 
-        q_grouped = sbuf("q_grouped", [P, D_PASSES, NQ, PACK], BF16, "q_then_pairs")
-        q_codes = sbuf("q_codes", [P, D_PASSES * NQ], U32)
-        q_scales = sbuf("q_scales", [P, D_PASSES * NQ], U8)
-        nc.scalar.copy(q_grouped[:], q_raw[:].rearrange("p o j w -> p o w j"))
-
-        pair_tags = ["pairs_then_vs", None, "q_then_pairs", None]
         k_pairs = {}
         k_parted = {}
 
         def gather_keys(g):
-            k_pairs[g] = sbuf("k_pairs%d" % g, [P, PAGE], U32, pair_tags[g])
+            k_pairs[g] = sbuf("k_pairs%d" % g, [P, PAGE], U32)
             nc.vector.tensor_copy(k_pairs[g][:], k_pool[:].indirect(page_offsets(g)))
 
         def part_keys(g):
-            k_parted[g] = sbuf("k_parted%d" % g, [P, D_PASSES, 2 * PAGE], U8)
+            k_parted[g] = sbuf("k_parted%d" % g, [P, D_PASSES, 2 * PAGE], U8, "parted%d" % g)
             nc.vector.tensor_copy(
                 k_parted[g][:].bitcast(U16),
                 k_pairs[g][:].bitcast(U16).rearrange("p (s o) -> p o s", o=D_PASSES),
@@ -122,18 +107,8 @@ def tile_attend_pkv4_soft_kb_gate_kernel(tc, qT, k_words, k_scales, v_words, v_s
         gather_keys(0)
         gather_keys(1)
         part_keys(0)
-        vs_pool = sbuf("vs_pool", [P, TOKENS], F32, "pairs_then_vs")
-        nc.sync.dma_start(vs_pool[:], vs)
-        v_pool = sbuf("v_pool", [P, POOL_PAGES * DV], U32, "q_then_v")
-        nc.sync.dma_start(
-            v_pool[:].bitcast(I32).rearrange("p (u e) -> p u e", u=POOL_PAGES),
-            v_words.rearrange("u p e r -> p u (e r)").bitcast(I32),
-        )
-        part_keys(1)
-        nc.vector.quantize_mx(
-            out=q_codes[:].bitcast(FP8X4), scales=q_scales[:], in_=q_grouped[:].rearrange("p o w j -> p (o w j)")
-        )
         gather_keys(2)
+        part_keys(1)
         gather_keys(3)
         part_keys(2)
         part_keys(3)
@@ -141,61 +116,86 @@ def tile_attend_pkv4_soft_kb_gate_kernel(tc, qT, k_words, k_scales, v_words, v_s
         raw_scores = [sbuf("raw_scores%d" % g, [P, PAGE], F32) for g in range(PAGES)]
         for g in range(PAGES):
             score_bank = bank("score_bank%d" % g, [P, PAGE], "bank%d" % g)
-            for o in range(D_PASSES):
+            for o in reversed(range(D_PASSES)):
                 nc.tensor.matmul_mx(
                     out=score_bank[:],
                     lhsT=q_codes[:, o * NQ : (o + 1) * NQ].bitcast(FP8X4),
                     lhsT_scale=q_scales[:, o * NQ : (o + 1) * NQ],
                     rhs=k_parted[g][:, o, :].bitcast(FP4X4),
                     rhs_scale=k_planes[:, o * SLOTS + g * PAGE : o * SLOTS + (g + 1) * PAGE],
-                    start=(o == 0),
-                    stop=(o == D_PASSES - 1),
+                    start=(o == D_PASSES - 1),
+                    stop=(o == 0),
                 )
             nc.scalar.copy(raw_scores[g][:], score_bank[:])
 
+        vs_pool = sbuf("vs_pool", [P, TOKENS], F32, "parted0")
+        nc.sync.dma_start(vs_pool[:], vs)
+        v_pool = sbuf("v_pool", [P, POOL_PAGES * DV], U32, "parted1")
+        nc.sync.dma_start(
+            v_pool[:].bitcast(I32).rearrange("p (u e) -> p u e", u=POOL_PAGES),
+            v_words.rearrange("u p e r -> p u (e r)").bitcast(I32),
+        )
+        og_sb = sbuf("og_sb", [P, DV], F32, "parted2")
+        nc.sync.dma_start(og_sb[:], og[0])
+        vsc_pool = sbuf("vsc_pool", [P, POOL_PAGES * DV], U8, "parted3")
+        nc.gpsimd.memset(vsc_pool[:].bitcast(I32), 0)
+        for quad in range(QUADRANTS):
+            nc.sync.dma_start(
+                vsc_pool[QUADRANT * quad : QUADRANT * quad + SCALE_ROWS, :].bitcast(I32).rearrange("f (u e) -> f u e", u=POOL_PAGES),
+                v_scales[:, SCALE_ROWS * quad : SCALE_ROWS * (quad + 1), :].bitcast(I32).rearrange("u f e -> f u e"),
+            )
+
         last = PAGES - 1
-        scores = [sbuf("scores%d" % g, [P, PAGE + (last if g == last else 0)], F32) for g in range(PAGES)]
+        scores = [sbuf("scores%d" % g, [P, PAGE], F32, "scores_then_tanh" if g == last else None) for g in range(PAGES)]
+        page_maxima = sbuf("page_maxima", [P, PAGES], F32, "maxima_then_plane")
         neg_max = sbuf("neg_max", [P, 1], F32)
 
         def add_bias(g):
             nc.vector.tensor_tensor(scores[g][:, :PAGE], kb_pool[:].indirect(page_offsets(g)), raw_scores[g][:], ALU.add)
 
         def page_max(g):
-            nc.vector.tensor_reduce(scores[last][:, PAGE + g : PAGE + g + 1], scores[g][:], AXIS_X, ALU.max)
+            nc.vector.tensor_reduce(page_maxima[:, g : g + 1], scores[g][:], AXIS_X, ALU.max)
 
         add_bias(0)
         for g in range(1, PAGES):
             add_bias(g)
             page_max(g - 1)
-        nc.vector.tensor_reduce(neg_max[:], scores[last][:], AXIS_X, ALU.max, negate=True)
+        page_max(last)
+        nc.vector.tensor_reduce(neg_max[:], page_maxima[:], AXIS_X, ALU.max, negate=True)
+        v_plane = sbuf("v_plane", [P, PAGES * DV], U8, "maxima_then_plane")
+        nc.vector.tensor_copy(v_plane[:], vsc_pool[:].indirect(v_offsets[:]))
 
-        probs = [sbuf("probs%d" % g, [P, PAGE], F32) for g in range(PAGES)]
+        probs = [sbuf("probs%d" % g, [P, PAGE], F32, "probs_then_codes" if g == last else None) for g in range(PAGES)]
         page_sum = sbuf("page_sum", [P, PAGES], F32)
         for g in range(PAGES):
             nc.scalar.activation(probs[g][:], scores[g][:, :PAGE], ACT.Exp, bias=neg_max[:], accum_out=page_sum[:, g : g + 1])
 
-        token_scale = [sbuf("token_scale%d" % g, [P, PAGE], F32) for g in range(PAGES)]
+        half_tanh = sbuf("half_tanh", [P, DV], F32, "scores_then_tanh")
+        gate = sbuf("gate", [P, DV], F32)
+        nc.scalar.activation(half_tanh[:], og_sb[:], ACT.Tanh, scale=0.5)
+        nc.scalar.activation(gate[:], half_tanh[:], ACT.Copy, scale=0.5, bias=0.5)
+
+        scaled = [sbuf("scaled%d" % g, [P, PAGE], F32) for g in range(PAGES)]
         dealt = [sbuf("dealt%d" % g, [P, 2, P, 2], BF16) for g in range(PAGES)]
         weights = [sbuf("weights%d" % g, [P, NQ, PACK], BF16) for g in range(PAGES)]
         w_codes = [sbuf("w_codes%d" % g, [P, NQ], U32) for g in range(PAGES)]
         w_scales = [sbuf("w_scales%d" % g, [P, NQ], U8) for g in range(PAGES)]
-        v_codes = sbuf("v_codes", [P, PAGES * DV], U32)
-        y_bank = bank("y_bank", [P, DV])
+
+        turned_banks = {}
 
         def gather_scale(g):
-            nc.vector.tensor_copy(token_scale[g][:], vs_pool[:].indirect(page_offsets(g)))
+            nc.vector.tensor_tensor(scaled[g][:], vs_pool[:].indirect(page_offsets(g)), probs[g][:], ALU.mult)
 
         def weigh(g):
-            nc.vector.tensor_tensor(
-                dealt[g][:],
-                probs[g][:].rearrange("p (s u e) -> p u s e", u=2, e=2),
-                token_scale[g][:].rearrange("p (s u e) -> p u s e", u=2, e=2),
-                ALU.mult,
-            )
+            nc.scalar.copy(dealt[g][:], scaled[g][:].rearrange("p (s u e) -> p u s e", u=2, e=2))
             turned = bank("turned%d" % g, [P, 2, NQ], "bank%d" % g)
             words = dealt[g][:].rearrange("p u s e -> p (u s e)").bitcast(F32)
             for u in range(2):
                 nc.tensor.transpose(turned[:, u, :], words[:, u * P : (u + 1) * P], identity[:])
+            turned_banks[g] = turned
+
+        def empty_bank(g):
+            turned = turned_banks[g]
             nc.scalar.copy(
                 weights[g][:].rearrange("p q r -> p (q r)").bitcast(F32).rearrange("p (q u) -> p q u", u=2),
                 turned[:].rearrange("p u q -> p q u"),
@@ -210,16 +210,20 @@ def tile_attend_pkv4_soft_kb_gate_kernel(tc, qT, k_words, k_scales, v_words, v_s
         for g in range(1, PAGES):
             gather_scale(g)
             weigh(g - 1)
-        weigh(last)
+            if g > 1:
+                empty_bank(g - 2)
         total = sbuf("total", [P, 1], F32)
         inv_total = sbuf("inv_total", [P, 1], F32)
         nc.vector.tensor_reduce(total[:], page_sum[:], AXIS_X, ALU.add)
-        quantise(0)
-        quantise(1)
-        nc.vector.reciprocal(inv_total[:], total[:])
+        weigh(last)
+        empty_bank(last - 1)
+        empty_bank(last)
+        v_codes = sbuf("v_codes", [P, PAGES * DV], U32, "probs_then_codes")
         nc.vector.tensor_copy(v_codes[:], v_pool[:].indirect(v_offsets[:]))
-        quantise(2)
-        quantise(3)
+        nc.vector.reciprocal(inv_total[:], total[:])
+        for g in range(PAGES):
+            quantise(g)
+        y_bank = bank("y_bank", [P, DV], "bank%d" % last)
         for g in range(PAGES):
             nc.tensor.matmul_mx(
                 out=y_bank[:],

@@ -49,52 +49,58 @@ def tile_attend_pkv4_soft_kb_gate_kernel(tc, qT, k_words, k_scales, v_words, v_s
             return offsets[:, g * cols : (g + 1) * cols]
 
         scale_rows = D_PASSES * QUADRANTS * SCALE_ROWS
-        ks_pool = sbuf("ks_pool", [P, TOKENS], U8, "ks_then_identity")
+        ks_pool = sbuf("ks_pool", [P, TOKENS], U8, "ks_then_kb")
         k_pool = sbuf("k_pool", [P, TOKENS], U32)
-        q_raw = sbuf("q_raw", [P, D_PASSES, PACK, NQ], F32)
+        q_raw = sbuf("q_raw", [P, D_PASSES, PACK, NQ], F32, "q_then_vs")
         nc.sync.dma_start(ks_pool[0:scale_rows, :].bitcast(I32), k_scales.bitcast(I32).rearrange("o f t -> (o f) t"))
         nc.sync.dma_start(offsets[:], offs)
+        nc.sync.dma_start(k_pool[:].bitcast(I32), k_words[0].rearrange("p t b -> p (t b)").bitcast(I32))
+        nc.sync.dma_start(v_offsets[:], voffs)
         nc.sync.dma_start(
             q_raw[:].rearrange("p o j w -> p o (j w)"),
             qT[0].rearrange("(o p j) w -> p o (j w)", o=D_PASSES, j=PACK),
         )
-        nc.sync.dma_start(k_pool[:].bitcast(I32), k_words[0].rearrange("p t b -> p (t b)").bitcast(I32))
-        nc.sync.dma_start(v_offsets[:], voffs)
-        kb_pool = sbuf("kb_pool", [P, TOKENS], F32)
-        nc.sync.dma_start(kb_pool[:], kb)
 
         k_planes = sbuf("k_planes", [P, D_PASSES * SLOTS], U8)
         nc.vector.memset(ks_pool[scale_rows : 2 * scale_rows, :].bitcast(I32), 0)
         nc.vector.memset(ks_pool[2 * scale_rows :, :].bitcast(I32), 0)
         nc.vector.memset(k_planes[:].bitcast(I32), 0)
 
-        q_grouped = sbuf("q_grouped", [P, D_PASSES, NQ, PACK], BF16)
+        og_sb = sbuf("og_sb", [P, DV], F32, "parted2")
+        nc.gpsimd.dma_start(og_sb[:], og[0])
+        half_tanh = sbuf("half_tanh", [P, DV], F32)
+        gate = sbuf("gate", [P, DV], F32)
+        nc.scalar.activation(half_tanh[:], og_sb[:], ACT.Tanh, scale=0.5)
+        nc.scalar.activation(gate[:], half_tanh[:], ACT.Copy, scale=0.5, bias=0.5)
+
+        q_grouped = sbuf("q_grouped", [P, D_PASSES, NQ, PACK], BF16, "q_then_pairs")
         q_codes = sbuf("q_codes", [P, D_PASSES * NQ], U32)
         q_scales = sbuf("q_scales", [P, D_PASSES * NQ], U8)
         nc.scalar.copy(q_grouped[:], q_raw[:].rearrange("p o j w -> p o w j"))
 
-        ks_rows = sbuf("ks_rows", [P, SLOTS], U8)
+        ks_rows = sbuf("ks_rows", [P, SLOTS], U8, "rows_then_identity")
         nc.vector.tensor_copy(ks_rows[:], ks_pool[:].indirect(offsets[:]))
         for o in range(D_PASSES):
             for quad in range(QUADRANTS):
                 first = SCALE_ROWS * (QUADRANTS * o + quad)
-                queue = nc.gpsimd if first == 0 else nc.scalar
+                queue = nc.gpsimd if first == 0 else nc.sync
                 queue.dma_start(
                     k_planes[QUADRANT * quad : QUADRANT * quad + SCALE_ROWS, o * SLOTS : (o + 1) * SLOTS].bitcast(I32),
                     ks_rows[first : first + SCALE_ROWS, :].bitcast(I32),
                 )
 
-        identity = sbuf("identity", [P, P], F32, "ks_then_identity")
+        kb_pool = sbuf("kb_pool", [P, TOKENS], F32, "ks_then_kb")
+        nc.sync.dma_start(kb_pool[:], kb)
+        vs_pool = sbuf("vs_pool", [P, TOKENS], F32, "q_then_vs")
+        nc.sync.dma_start(vs_pool[:], vs)
+        identity = sbuf("identity", [P, P], F32, "rows_then_identity")
         make_identity(nc, identity[:])
-        nc.vector.quantize_mx(
-            out=q_codes[:].bitcast(FP8X4), scales=q_scales[:], in_=q_grouped[:].rearrange("p o w j -> p (o w j)")
-        )
 
         k_pairs = {}
         k_parted = {}
 
         def gather_keys(g):
-            k_pairs[g] = sbuf("k_pairs%d" % g, [P, PAGE], U32)
+            k_pairs[g] = sbuf("k_pairs%d" % g, [P, PAGE], U32, {0: "pairs_vsc_scaled", 2: "q_then_pairs"}.get(g))
             nc.vector.tensor_copy(k_pairs[g][:], k_pool[:].indirect(page_offsets(g)))
 
         def part_keys(g):
@@ -107,8 +113,18 @@ def tile_attend_pkv4_soft_kb_gate_kernel(tc, qT, k_words, k_scales, v_words, v_s
         gather_keys(0)
         gather_keys(1)
         part_keys(0)
-        gather_keys(2)
+        vsc_pool = sbuf("vsc_pool", [P, POOL_PAGES * DV], U8, "pairs_vsc_scaled")
+        nc.gpsimd.memset(vsc_pool[:].bitcast(I32), 0)
+        for quad in range(QUADRANTS):
+            nc.gpsimd.dma_start(
+                vsc_pool[QUADRANT * quad : QUADRANT * quad + SCALE_ROWS, :].bitcast(I32).rearrange("f (u e) -> f u e", u=POOL_PAGES),
+                v_scales[:, SCALE_ROWS * quad : SCALE_ROWS * (quad + 1), :].bitcast(I32).rearrange("u f e -> f u e"),
+            )
         part_keys(1)
+        nc.vector.quantize_mx(
+            out=q_codes[:].bitcast(FP8X4), scales=q_scales[:], in_=q_grouped[:].rearrange("p o w j -> p (o w j)")
+        )
+        gather_keys(2)
         gather_keys(3)
         part_keys(2)
         part_keys(3)
@@ -128,25 +144,14 @@ def tile_attend_pkv4_soft_kb_gate_kernel(tc, qT, k_words, k_scales, v_words, v_s
                 )
             nc.scalar.copy(raw_scores[g][:], score_bank[:])
 
-        vs_pool = sbuf("vs_pool", [P, TOKENS], F32, "parted0")
-        nc.sync.dma_start(vs_pool[:], vs)
         v_pool = sbuf("v_pool", [P, POOL_PAGES * DV], U32, "parted1")
         nc.sync.dma_start(
             v_pool[:].bitcast(I32).rearrange("p (u e) -> p u e", u=POOL_PAGES),
             v_words.rearrange("u p e r -> p u (e r)").bitcast(I32),
         )
-        og_sb = sbuf("og_sb", [P, DV], F32, "parted2")
-        nc.sync.dma_start(og_sb[:], og[0])
-        vsc_pool = sbuf("vsc_pool", [P, POOL_PAGES * DV], U8, "parted3")
-        nc.gpsimd.memset(vsc_pool[:].bitcast(I32), 0)
-        for quad in range(QUADRANTS):
-            nc.sync.dma_start(
-                vsc_pool[QUADRANT * quad : QUADRANT * quad + SCALE_ROWS, :].bitcast(I32).rearrange("f (u e) -> f u e", u=POOL_PAGES),
-                v_scales[:, SCALE_ROWS * quad : SCALE_ROWS * (quad + 1), :].bitcast(I32).rearrange("u f e -> f u e"),
-            )
 
         last = PAGES - 1
-        scores = [sbuf("scores%d" % g, [P, PAGE], F32, "scores_then_tanh" if g == last else None) for g in range(PAGES)]
+        scores = [sbuf("scores%d" % g, [P, PAGE], F32) for g in range(PAGES)]
         page_maxima = sbuf("page_maxima", [P, PAGES], F32, "maxima_then_plane")
         neg_max = sbuf("neg_max", [P, 1], F32)
 
@@ -170,12 +175,7 @@ def tile_attend_pkv4_soft_kb_gate_kernel(tc, qT, k_words, k_scales, v_words, v_s
         for g in range(PAGES):
             nc.scalar.activation(probs[g][:], scores[g][:, :PAGE], ACT.Exp, bias=neg_max[:], accum_out=page_sum[:, g : g + 1])
 
-        half_tanh = sbuf("half_tanh", [P, DV], F32, "scores_then_tanh")
-        gate = sbuf("gate", [P, DV], F32)
-        nc.scalar.activation(half_tanh[:], og_sb[:], ACT.Tanh, scale=0.5)
-        nc.scalar.activation(gate[:], half_tanh[:], ACT.Copy, scale=0.5, bias=0.5)
-
-        scaled = [sbuf("scaled%d" % g, [P, PAGE], F32) for g in range(PAGES)]
+        scaled = [sbuf("scaled%d" % g, [P, PAGE], F32, "pairs_vsc_scaled" if g == 0 else None) for g in range(PAGES)]
         dealt = [sbuf("dealt%d" % g, [P, 2, P, 2], BF16) for g in range(PAGES)]
         weights = [sbuf("weights%d" % g, [P, NQ, PACK], BF16) for g in range(PAGES)]
         w_codes = [sbuf("w_codes%d" % g, [P, NQ], U32) for g in range(PAGES)]
@@ -223,7 +223,7 @@ def tile_attend_pkv4_soft_kb_gate_kernel(tc, qT, k_words, k_scales, v_words, v_s
         nc.vector.reciprocal(inv_total[:], total[:])
         for g in range(PAGES):
             quantise(g)
-        y_bank = bank("y_bank", [P, DV], "bank%d" % last)
+        y_bank = bank("y_bank", [P, DV], "bank%d" % (last - 1))
         for g in range(PAGES):
             nc.tensor.matmul_mx(
                 out=y_bank[:],

@@ -25,6 +25,8 @@ D_PASSES = D // (P * PACK)
 QUADRANTS, QUADRANT = 4, 32
 SCALE_ROWS = 4
 LIST_ROWS = 16
+HALVES = 2
+FP4_WORD_BYTES = 2
 
 FLOPS = 2 * NQ * SLOTS * (D + DV)
 
@@ -49,10 +51,11 @@ def tile_attend_pkv4_soft_kb_gate_kernel(tc, qT, k_words, k_scales, v_words, v_s
             return offsets[:, g * cols : (g + 1) * cols]
 
         scale_rows = D_PASSES * QUADRANTS * SCALE_ROWS
+        rows_from = P - scale_rows
         ks_pool = sbuf("ks_pool", [P, TOKENS], U8, "ks_then_kb")
         k_pool = sbuf("k_pool", [P, TOKENS], U32)
         q_raw = sbuf("q_raw", [P, D_PASSES, PACK, NQ], F32, "q_then_vs")
-        nc.sync.dma_start(ks_pool[0:scale_rows, :].bitcast(I32), k_scales.bitcast(I32).rearrange("o f t -> (o f) t"))
+        nc.sync.dma_start(ks_pool[rows_from:, :].bitcast(I32), k_scales.bitcast(I32).rearrange("o f t -> (o f) t"))
         nc.sync.dma_start(offsets[:], offs)
         nc.sync.dma_start(k_pool[:].bitcast(I32), k_words[0].rearrange("p t b -> p (t b)").bitcast(I32))
         nc.sync.dma_start(v_offsets[:], voffs)
@@ -62,11 +65,10 @@ def tile_attend_pkv4_soft_kb_gate_kernel(tc, qT, k_words, k_scales, v_words, v_s
         )
 
         k_planes = sbuf("k_planes", [P, D_PASSES * SLOTS], U8)
-        nc.vector.memset(ks_pool[scale_rows : 2 * scale_rows, :].bitcast(I32), 0)
-        nc.vector.memset(ks_pool[2 * scale_rows :, :].bitcast(I32), 0)
+        nc.vector.memset(ks_pool[:rows_from, :].bitcast(I32), 0)
         nc.vector.memset(k_planes[:].bitcast(I32), 0)
 
-        og_sb = sbuf("og_sb", [P, DV], F32, "parted2")
+        og_sb = sbuf("og_sb", [P, DV], F32)
         nc.gpsimd.dma_start(og_sb[:], og[0])
         half_tanh = sbuf("half_tanh", [P, DV], F32)
         gate = sbuf("gate", [P, DV], F32)
@@ -83,10 +85,10 @@ def tile_attend_pkv4_soft_kb_gate_kernel(tc, qT, k_words, k_scales, v_words, v_s
         for o in range(D_PASSES):
             for quad in range(QUADRANTS):
                 first = SCALE_ROWS * (QUADRANTS * o + quad)
-                queue = nc.gpsimd if first == 0 else nc.sync
+                queue = nc.gpsimd if first == scale_rows - SCALE_ROWS else nc.sync
                 queue.dma_start(
                     k_planes[QUADRANT * quad : QUADRANT * quad + SCALE_ROWS, o * SLOTS : (o + 1) * SLOTS].bitcast(I32),
-                    ks_rows[first : first + SCALE_ROWS, :].bitcast(I32),
+                    ks_rows[rows_from + first : rows_from + first + SCALE_ROWS, :].bitcast(I32),
                 )
 
         kb_pool = sbuf("kb_pool", [P, TOKENS], F32, "ks_then_kb")
@@ -96,20 +98,21 @@ def tile_attend_pkv4_soft_kb_gate_kernel(tc, qT, k_words, k_scales, v_words, v_s
         identity = sbuf("identity", [P, P], F32, "rows_then_identity")
         make_identity(nc, identity[:])
 
-        k_pairs = {}
         k_parted = {}
 
         def gather_keys(g):
-            k_pairs[g] = sbuf("k_pairs%d" % g, [P, PAGE], U32, {0: "pairs_vsc_scaled", 2: "q_then_pairs"}.get(g))
-            nc.vector.tensor_copy(k_pairs[g][:], k_pool[:].indirect(page_offsets(g)))
+            nc.vector.tensor_copy(k_pairs[g], k_pool[:].indirect(page_offsets(g)))
 
         def part_keys(g):
-            k_parted[g] = sbuf("k_parted%d" % g, [P, D_PASSES, 2 * PAGE], U8, "parted%d" % g)
+            k_parted[g] = sbuf("k_parted%d" % g, [P, D_PASSES, FP4_WORD_BYTES * PAGE], U8, "parted%d" % g)
             nc.vector.tensor_copy(
                 k_parted[g][:].bitcast(U16),
-                k_pairs[g][:].bitcast(U16).rearrange("p (s o) -> p o s", o=D_PASSES),
+                k_pairs[g].bitcast(U16).rearrange("p (s o) -> p o s", o=D_PASSES),
             )
 
+        first_pairs = sbuf("first_pairs", [P, PAGE], U32, "pairs_vsc_scaled")
+        second_pairs = sbuf("second_pairs", [P, PAGE], U32)
+        k_pairs = [first_pairs[:], second_pairs[:]]
         gather_keys(0)
         gather_keys(1)
         part_keys(0)
@@ -124,6 +127,8 @@ def tile_attend_pkv4_soft_kb_gate_kernel(tc, qT, k_words, k_scales, v_words, v_s
         nc.vector.quantize_mx(
             out=q_codes[:].bitcast(FP8X4), scales=q_scales[:], in_=q_grouped[:].rearrange("p o w j -> p (o w j)")
         )
+        late_pairs = sbuf("late_pairs", [P, 2, PAGE], U32, "q_then_pairs")
+        k_pairs.extend([late_pairs[:, 0, :], late_pairs[:, 1, :]])
         gather_keys(2)
         gather_keys(3)
         part_keys(2)
@@ -151,53 +156,61 @@ def tile_attend_pkv4_soft_kb_gate_kernel(tc, qT, k_words, k_scales, v_words, v_s
         )
 
         last = PAGES - 1
-        scores = [sbuf("scores%d" % g, [P, PAGE], F32) for g in range(PAGES)]
-        page_maxima = sbuf("page_maxima", [P, PAGES], F32, "maxima_then_plane")
+        half = SLOTS // 2
+        scores = sbuf("scores", [P, SLOTS], F32)
+        neg_late = sbuf("neg_late", [P, half], F32)
+        neg_early_max = sbuf("neg_early_max", [P, 1], F32, "maximum_then_plane")
         neg_max = sbuf("neg_max", [P, 1], F32)
 
         def add_bias(g):
-            nc.vector.tensor_tensor(scores[g][:, :PAGE], kb_pool[:].indirect(page_offsets(g)), raw_scores[g][:], ALU.add)
+            nc.vector.tensor_tensor(
+                scores[:, g * PAGE : (g + 1) * PAGE], kb_pool[:].indirect(page_offsets(g)), raw_scores[g][:], ALU.add
+            )
 
-        def page_max(g):
-            nc.vector.tensor_reduce(page_maxima[:, g : g + 1], scores[g][:], AXIS_X, ALU.max)
-
-        add_bias(0)
-        for g in range(1, PAGES):
+        for g in range(last):
             add_bias(g)
-            page_max(g - 1)
-        page_max(last)
-        nc.vector.tensor_reduce(neg_max[:], page_maxima[:], AXIS_X, ALU.max, negate=True)
-        v_plane = sbuf("v_plane", [P, PAGES * DV], U8, "maxima_then_plane")
+        nc.vector.tensor_reduce(neg_early_max[:], scores[:, :half], AXIS_X, ALU.max, negate=True)
+        add_bias(last)
+        nc.vector.tensor_scalar(
+            neg_late[:], scores[:, half:], -1.0, neg_early_max[:], ALU.mult, ALU.min, accum_out=neg_max[:]
+        )
+        v_plane = sbuf("v_plane", [P, PAGES * DV], U8, "maximum_then_plane")
         nc.vector.tensor_copy(v_plane[:], vsc_pool[:].indirect(v_offsets[:]))
 
         probs = [sbuf("probs%d" % g, [P, PAGE], F32, "probs_then_codes" if g == last else None) for g in range(PAGES)]
         page_sum = sbuf("page_sum", [P, PAGES], F32)
         for g in range(PAGES):
-            nc.scalar.activation(probs[g][:], scores[g][:, :PAGE], ACT.Exp, bias=neg_max[:], accum_out=page_sum[:, g : g + 1])
+            start = g * PAGE
+            if start < half:
+                source, sign = scores[:, start : start + PAGE], 1.0
+            else:
+                source, sign = neg_late[:, start - half : start - half + PAGE], -1.0
+            nc.scalar.activation(probs[g][:], source, ACT.Exp, bias=neg_max[:], scale=sign, accum_out=page_sum[:, g : g + 1])
+        total = sbuf("total", [P, 1], F32)
 
         scaled = [sbuf("scaled%d" % g, [P, PAGE], F32, "pairs_vsc_scaled" if g == 0 else None) for g in range(PAGES)]
-        dealt = [sbuf("dealt%d" % g, [P, 2, P, 2], BF16) for g in range(PAGES)]
+        dealt = [sbuf("dealt%d" % g, [P, HALVES, P, HALVES], BF16) for g in range(PAGES)]
         weights = [sbuf("weights%d" % g, [P, NQ, PACK], BF16) for g in range(PAGES)]
         w_codes = [sbuf("w_codes%d" % g, [P, NQ], U32) for g in range(PAGES)]
         w_scales = [sbuf("w_scales%d" % g, [P, NQ], U8) for g in range(PAGES)]
 
         turned_banks = {}
 
-        def gather_scale(g):
+        def scale_probs(g):
             nc.vector.tensor_tensor(scaled[g][:], vs_pool[:].indirect(page_offsets(g)), probs[g][:], ALU.mult)
 
         def weigh(g):
-            nc.scalar.copy(dealt[g][:], scaled[g][:].rearrange("p (s u e) -> p u s e", u=2, e=2))
-            turned = bank("turned%d" % g, [P, 2, NQ], "bank%d" % g)
+            nc.scalar.copy(dealt[g][:], scaled[g][:].rearrange("p (s u e) -> p u s e", u=HALVES, e=HALVES))
+            turned = bank("turned%d" % g, [P, HALVES, NQ], "bank%d" % g)
             words = dealt[g][:].rearrange("p u s e -> p (u s e)").bitcast(F32)
-            for u in range(2):
+            for u in range(HALVES):
                 nc.tensor.transpose(turned[:, u, :], words[:, u * P : (u + 1) * P], identity[:])
             turned_banks[g] = turned
 
         def empty_bank(g):
             turned = turned_banks[g]
             nc.scalar.copy(
-                weights[g][:].rearrange("p q r -> p (q r)").bitcast(F32).rearrange("p (q u) -> p q u", u=2),
+                weights[g][:].rearrange("p q r -> p (q r)").bitcast(F32).rearrange("p (q u) -> p q u", u=HALVES),
                 turned[:].rearrange("p u q -> p q u"),
             )
 
@@ -206,13 +219,12 @@ def tile_attend_pkv4_soft_kb_gate_kernel(tc, qT, k_words, k_scales, v_words, v_s
                 out=w_codes[g][:].bitcast(FP8X4), scales=w_scales[g][:], in_=weights[g][:].rearrange("p q r -> p (q r)")
             )
 
-        gather_scale(0)
+        scale_probs(0)
         for g in range(1, PAGES):
-            gather_scale(g)
+            scale_probs(g)
             weigh(g - 1)
             if g > 1:
                 empty_bank(g - 2)
-        total = sbuf("total", [P, 1], F32)
         inv_total = sbuf("inv_total", [P, 1], F32)
         nc.vector.tensor_reduce(total[:], page_sum[:], AXIS_X, ALU.add)
         weigh(last)

@@ -35,6 +35,7 @@ def tile_attend_pkv4_soft_kb_gate_kernel(tc, qT, k_words, k_scales, v_words, v_s
     nc = tc.nc
     with ExitStack() as ctx:
         keep = ctx.enter_context(tc.tile_pool(name="keep", bufs=1))
+        windows = ctx.enter_context(tc.tile_pool(name="windows", bufs=1))
         psum = ctx.enter_context(tc.psum_pool(name="psum", bufs=1))
 
         def sbuf(name, shape, dtype, tag=None):
@@ -46,26 +47,35 @@ def tile_attend_pkv4_soft_kb_gate_kernel(tc, qT, k_words, k_scales, v_words, v_s
         offsets = keep.tile([P, SLOTS // LIST_ROWS], U16, name="offsets")
         v_offsets = keep.tile([P, PAGES * DV // LIST_ROWS], U16, name="v_offsets")
         cols = PAGE // LIST_ROWS
+        last = PAGES - 1
 
         def page_offsets(g):
             return offsets[:, g * cols : (g + 1) * cols]
 
-        scale_rows = D_PASSES * QUADRANTS * SCALE_ROWS
-        rows_from = P - scale_rows
-        ks_pool = sbuf("ks_pool", [P, TOKENS], U8, "ks_then_kb")
+        def quadrant(quad, rows=QUADRANT):
+            return slice(QUADRANT * quad, QUADRANT * quad + rows)
+
+        row_bytes = 4 * TOKENS
+        ks_pool = windows.tile([P, TOKENS], U8, name="ks_pool", offset=row_bytes - TOKENS // 2)
         k_pool = sbuf("k_pool", [P, TOKENS], U32)
-        q_raw = sbuf("q_raw", [P, D_PASSES, PACK, NQ], F32, "q_then_vs")
-        nc.sync.dma_start(ks_pool[rows_from:, :].bitcast(I32), k_scales.bitcast(I32).rearrange("o f t -> (o f) t"))
+        q_raw = sbuf("q_raw", [P, D_PASSES, PACK, NQ], F32)
+        scale_rows = k_scales.bitcast(I32).rearrange("o f t -> (o f) t")
+        nc.sync.dma_start(ks_pool[quadrant(0), :].bitcast(I32), scale_rows)
+        nc.sync.dma_start(
+            ks_pool[quadrant(QUADRANTS - 1), :].bitcast(I32),
+            scale_rows[QUADRANT - SCALE_ROWS :, :].unsqueeze(0).to_broadcast([QUADRANT // SCALE_ROWS, SCALE_ROWS, TOKENS // 4]),
+        )
         nc.sync.dma_start(offsets[:], offs)
-        nc.sync.dma_start(k_pool[:].bitcast(I32), k_words[0].rearrange("p t b -> p (t b)").bitcast(I32))
         nc.sync.dma_start(v_offsets[:], voffs)
         nc.sync.dma_start(
             q_raw[:].rearrange("p o j w -> p o (j w)"),
             qT[0].rearrange("(o p j) w -> p o (j w)", o=D_PASSES, j=PACK),
         )
+        nc.sync.dma_start(k_pool[:].bitcast(I32), k_words[0].rearrange("p t b -> p (t b)").bitcast(I32))
 
         k_planes = sbuf("k_planes", [P, D_PASSES * SLOTS], U8)
-        nc.vector.memset(ks_pool[:rows_from, :].bitcast(I32), 0)
+        for quad in range(1, QUADRANTS - 1):
+            nc.vector.memset(ks_pool[quadrant(quad), :].bitcast(I32), 0)
         nc.vector.memset(k_planes[:].bitcast(I32), 0)
 
         og_sb = sbuf("og_sb", [P, DV], F32)
@@ -75,64 +85,66 @@ def tile_attend_pkv4_soft_kb_gate_kernel(tc, qT, k_words, k_scales, v_words, v_s
         nc.scalar.activation(half_tanh[:], og_sb[:], ACT.Tanh, scale=0.5)
         nc.scalar.activation(gate[:], half_tanh[:], ACT.Copy, scale=0.5, bias=0.5)
 
-        q_grouped = sbuf("q_grouped", [P, D_PASSES, NQ, PACK], BF16, "q_then_pairs")
+        vsc_pool = sbuf("vsc_pool", [P, POOL_PAGES * DV], U8)
+        nc.gpsimd.memset(vsc_pool[:].bitcast(I32), 0)
+        for quad in range(QUADRANTS):
+            nc.gpsimd.dma_start(
+                vsc_pool[quadrant(quad, SCALE_ROWS), :].bitcast(I32).rearrange("f (u e) -> f u e", u=POOL_PAGES),
+                v_scales[:, SCALE_ROWS * quad : SCALE_ROWS * (quad + 1), :].bitcast(I32).rearrange("u f e -> f u e"),
+            )
+        identity = sbuf("identity", [P, P], F32)
+        make_identity(nc, identity[:])
+
+        q_grouped = sbuf("q_grouped", [P, D_PASSES, NQ, PACK], BF16)
         q_codes = sbuf("q_codes", [P, D_PASSES * NQ], U32)
         q_scales = sbuf("q_scales", [P, D_PASSES * NQ], U8)
         nc.scalar.copy(q_grouped[:], q_raw[:].rearrange("p o j w -> p o w j"))
 
-        ks_rows = sbuf("ks_rows", [P, SLOTS], U8, "rows_then_identity")
+        ks_rows = sbuf("ks_rows", [P, SLOTS], U8, "rows_then_v")
         nc.vector.tensor_copy(ks_rows[:], ks_pool[:].indirect(offsets[:]))
+        in_place = ((0, 0), (D_PASSES - 1, QUADRANTS - 1))
         for o in range(D_PASSES):
             for quad in range(QUADRANTS):
-                first = SCALE_ROWS * (QUADRANTS * o + quad)
-                queue = nc.gpsimd if first == scale_rows - SCALE_ROWS else nc.sync
-                queue.dma_start(
-                    k_planes[QUADRANT * quad : QUADRANT * quad + SCALE_ROWS, o * SLOTS : (o + 1) * SLOTS].bitcast(I32),
-                    ks_rows[rows_from + first : rows_from + first + SCALE_ROWS, :].bitcast(I32),
-                )
+                target = k_planes[quadrant(quad, SCALE_ROWS), o * SLOTS : (o + 1) * SLOTS].bitcast(I32)
+                if (o, quad) in in_place:
+                    nc.vector.tensor_copy(target, ks_rows[quadrant(quad, SCALE_ROWS), :].bitcast(I32))
+                else:
+                    first = SCALE_ROWS * (QUADRANTS * o + quad)
+                    nc.sync.dma_start(target, ks_rows[first : first + SCALE_ROWS, :].bitcast(I32))
 
-        kb_pool = sbuf("kb_pool", [P, TOKENS], F32, "ks_then_kb")
+        kb_pool = windows.tile([P, TOKENS], F32, name="kb_pool", offset=0)
         nc.sync.dma_start(kb_pool[:], kb)
-        vs_pool = sbuf("vs_pool", [P, TOKENS], F32, "q_then_vs")
+        vs_pool = windows.tile([P, TOKENS], F32, name="vs_pool", offset=row_bytes)
         nc.sync.dma_start(vs_pool[:], vs)
-        identity = sbuf("identity", [P, P], F32, "rows_then_identity")
-        make_identity(nc, identity[:])
+        v_pool = sbuf("v_pool", [P, POOL_PAGES * DV], U32, "rows_then_v")
+        nc.sync.dma_start(
+            v_pool[:].bitcast(I32).rearrange("p (u e) -> p u e", u=POOL_PAGES),
+            v_words.rearrange("u p e r -> p u (e r)").bitcast(I32),
+        )
 
-        k_parted = {}
-
-        def gather_keys(g):
-            nc.vector.tensor_copy(k_pairs[g], k_pool[:].indirect(page_offsets(g)))
-
-        def part_keys(g):
-            k_parted[g] = sbuf("k_parted%d" % g, [P, D_PASSES, FP4_WORD_BYTES * PAGE], U8, "parted%d" % g)
-            nc.vector.tensor_copy(
-                k_parted[g][:].bitcast(U16),
-                k_pairs[g].bitcast(U16).rearrange("p (s o) -> p o s", o=D_PASSES),
-            )
-
-        first_pairs = sbuf("first_pairs", [P, PAGE], U32, "pairs_vsc_scaled")
-        second_pairs = sbuf("second_pairs", [P, PAGE], U32)
-        k_pairs = [first_pairs[:], second_pairs[:]]
-        gather_keys(0)
-        gather_keys(1)
-        part_keys(0)
-        vsc_pool = sbuf("vsc_pool", [P, POOL_PAGES * DV], U8, "pairs_vsc_scaled")
-        nc.gpsimd.memset(vsc_pool[:].bitcast(I32), 0)
-        for quad in range(QUADRANTS):
-            nc.gpsimd.dma_start(
-                vsc_pool[QUADRANT * quad : QUADRANT * quad + SCALE_ROWS, :].bitcast(I32).rearrange("f (u e) -> f u e", u=POOL_PAGES),
-                v_scales[:, SCALE_ROWS * quad : SCALE_ROWS * (quad + 1), :].bitcast(I32).rearrange("u f e -> f u e"),
-            )
-        part_keys(1)
         nc.vector.quantize_mx(
             out=q_codes[:].bitcast(FP8X4), scales=q_scales[:], in_=q_grouped[:].rearrange("p o w j -> p (o w j)")
         )
-        late_pairs = sbuf("late_pairs", [P, 2, PAGE], U32, "q_then_pairs")
-        k_pairs.extend([late_pairs[:, 0, :], late_pairs[:, 1, :]])
-        gather_keys(2)
-        gather_keys(3)
-        part_keys(2)
-        part_keys(3)
+        v_plane = sbuf("v_plane", [P, PAGES * DV], U8)
+        nc.vector.tensor_copy(v_plane[:], vsc_pool[:].indirect(v_offsets[:]))
+
+        k_pairs = [sbuf("k_pairs%d" % g, [P, PAGE], U32) for g in range(PAGES)]
+        k_parted = [sbuf("k_parted%d" % g, [P, D_PASSES, FP4_WORD_BYTES * PAGE], U8) for g in range(PAGES)]
+
+        def gather_keys(g):
+            nc.vector.tensor_copy(k_pairs[g][:], k_pool[:].indirect(page_offsets(g)))
+
+        def part_keys(g):
+            nc.vector.tensor_copy(
+                k_parted[g][:].bitcast(U16),
+                k_pairs[g][:].bitcast(U16).rearrange("p (s o) -> p o s", o=D_PASSES),
+            )
+
+        gather_keys(0)
+        for g in range(1, PAGES):
+            gather_keys(g)
+            part_keys(g - 1)
+        part_keys(last)
 
         raw_scores = [sbuf("raw_scores%d" % g, [P, PAGE], F32) for g in range(PAGES)]
         for g in range(PAGES):
@@ -149,58 +161,44 @@ def tile_attend_pkv4_soft_kb_gate_kernel(tc, qT, k_words, k_scales, v_words, v_s
                 )
             nc.scalar.copy(raw_scores[g][:], score_bank[:])
 
-        v_pool = sbuf("v_pool", [P, POOL_PAGES * DV], U32, "parted1")
-        nc.sync.dma_start(
-            v_pool[:].bitcast(I32).rearrange("p (u e) -> p u e", u=POOL_PAGES),
-            v_words.rearrange("u p e r -> p u (e r)").bitcast(I32),
-        )
-
-        last = PAGES - 1
-        half = SLOTS // 2
-        scores = sbuf("scores", [P, SLOTS], F32)
-        neg_late = sbuf("neg_late", [P, half], F32)
-        neg_early_max = sbuf("neg_early_max", [P, 1], F32, "maximum_then_plane")
-        neg_max = sbuf("neg_max", [P, 1], F32)
+        scores = [sbuf("scores%d" % g, [P, PAGE], F32) for g in range(PAGES)]
+        probs = [sbuf("probs%d" % g, [P, PAGE], F32) for g in range(PAGES)]
+        neg_page_max = sbuf("neg_page_max", [P, PAGES], F32)
+        page_sum = sbuf("page_sum", [P, PAGES], F32)
 
         def add_bias(g):
-            nc.vector.tensor_tensor(
-                scores[:, g * PAGE : (g + 1) * PAGE], kb_pool[:].indirect(page_offsets(g)), raw_scores[g][:], ALU.add
+            nc.vector.tensor_tensor(scores[g][:], kb_pool[:].indirect(page_offsets(g)), raw_scores[g][:], ALU.add)
+
+        def page_softmax(g):
+            nc.vector.tensor_reduce(neg_page_max[:, g : g + 1], scores[g][:], AXIS_X, ALU.max, negate=True)
+            nc.scalar.activation(
+                probs[g][:], scores[g][:], ACT.Exp, bias=neg_page_max[:, g : g + 1], accum_out=page_sum[:, g : g + 1]
             )
 
-        for g in range(last):
+        add_bias(0)
+        for g in range(1, PAGES):
             add_bias(g)
-        nc.vector.tensor_reduce(neg_early_max[:], scores[:, :half], AXIS_X, ALU.max, negate=True)
-        add_bias(last)
-        nc.vector.tensor_scalar(
-            neg_late[:], scores[:, half:], -1.0, neg_early_max[:], ALU.mult, ALU.min, accum_out=neg_max[:]
-        )
-        v_plane = sbuf("v_plane", [P, PAGES * DV], U8, "maximum_then_plane")
-        nc.vector.tensor_copy(v_plane[:], vsc_pool[:].indirect(v_offsets[:]))
+            page_softmax(g - 1)
+        page_softmax(last)
 
-        probs = [sbuf("probs%d" % g, [P, PAGE], F32, "probs_then_codes" if g == last else None) for g in range(PAGES)]
-        page_sum = sbuf("page_sum", [P, PAGES], F32)
-        for g in range(PAGES):
-            start = g * PAGE
-            if start < half:
-                source, sign = scores[:, start : start + PAGE], 1.0
-            else:
-                source, sign = neg_late[:, start - half : start - half + PAGE], -1.0
-            nc.scalar.activation(probs[g][:], source, ACT.Exp, bias=neg_max[:], scale=sign, accum_out=page_sum[:, g : g + 1])
-        total = sbuf("total", [P, 1], F32)
-
-        scaled = [sbuf("scaled%d" % g, [P, PAGE], F32, "pairs_vsc_scaled" if g == 0 else None) for g in range(PAGES)]
+        scaled = [sbuf("scaled%d" % g, [P, PAGE], F32) for g in range(PAGES)]
         dealt = [sbuf("dealt%d" % g, [P, HALVES, P, HALVES], BF16) for g in range(PAGES)]
         weights = [sbuf("weights%d" % g, [P, NQ, PACK], BF16) for g in range(PAGES)]
         w_codes = [sbuf("w_codes%d" % g, [P, NQ], U32) for g in range(PAGES)]
         w_scales = [sbuf("w_scales%d" % g, [P, NQ], U8) for g in range(PAGES)]
-
+        neg_max = sbuf("neg_max", [P, 1], F32)
+        rescale = sbuf("rescale", [P, PAGES], F32)
         turned_banks = {}
 
         def scale_probs(g):
             nc.vector.tensor_tensor(scaled[g][:], vs_pool[:].indirect(page_offsets(g)), probs[g][:], ALU.mult)
 
         def weigh(g):
-            nc.scalar.copy(dealt[g][:], scaled[g][:].rearrange("p (s u e) -> p u s e", u=HALVES, e=HALVES))
+            source = scaled[g][:].rearrange("p (s u e) -> p u s e", u=HALVES, e=HALVES)
+            if g == last:
+                nc.vector.tensor_scalar(dealt[g][:], source, rescale[:, g : g + 1], None, ALU.mult)
+            else:
+                nc.scalar.activation(dealt[g][:], source, ACT.Copy, scale=rescale[:, g : g + 1])
             turned = bank("turned%d" % g, [P, HALVES, NQ], "bank%d" % g)
             words = dealt[g][:].rearrange("p u s e -> p (u s e)").bitcast(F32)
             for u in range(HALVES):
@@ -208,10 +206,9 @@ def tile_attend_pkv4_soft_kb_gate_kernel(tc, qT, k_words, k_scales, v_words, v_s
             turned_banks[g] = turned
 
         def empty_bank(g):
-            turned = turned_banks[g]
             nc.scalar.copy(
                 weights[g][:].rearrange("p q r -> p (q r)").bitcast(F32).rearrange("p (q u) -> p q u", u=HALVES),
-                turned[:].rearrange("p u q -> p q u"),
+                turned_banks[g][:].rearrange("p u q -> p q u"),
             )
 
         def quantise(g):
@@ -220,17 +217,20 @@ def tile_attend_pkv4_soft_kb_gate_kernel(tc, qT, k_words, k_scales, v_words, v_s
             )
 
         scale_probs(0)
+        nc.vector.tensor_reduce(neg_max[:], neg_page_max[:], AXIS_X, ALU.min)
+        nc.scalar.activation(rescale[:], neg_page_max[:], ACT.Exp, bias=neg_max[:], scale=-1.0)
         for g in range(1, PAGES):
             scale_probs(g)
-            weigh(g - 1)
-            if g > 1:
-                empty_bank(g - 2)
+        for g in range(last):
+            weigh(g)
+        rescaled_sum = sbuf("rescaled_sum", [P, PAGES], F32)
+        total = sbuf("total", [P, 1], F32)
         inv_total = sbuf("inv_total", [P, 1], F32)
-        nc.vector.tensor_reduce(total[:], page_sum[:], AXIS_X, ALU.add)
+        nc.vector.scalar_tensor_tensor(rescaled_sum[:], page_sum[:], 1.0, rescale[:], ALU.mult, ALU.mult, accum_out=total[:])
         weigh(last)
-        empty_bank(last - 1)
-        empty_bank(last)
-        v_codes = sbuf("v_codes", [P, PAGES * DV], U32, "probs_then_codes")
+        for g in range(PAGES):
+            empty_bank(g)
+        v_codes = sbuf("v_codes", [P, PAGES * DV], U32)
         nc.vector.tensor_copy(v_codes[:], v_pool[:].indirect(v_offsets[:]))
         nc.vector.reciprocal(inv_total[:], total[:])
         for g in range(PAGES):

@@ -26,6 +26,7 @@ QUADRANTS, QUADRANT = 4, 32
 SCALE_ROWS = 4
 LIST_ROWS = 16
 HALVES = 2
+LATE_BORDER = POOL_PAGES * DV
 FP4_WORD_BYTES = 2
 
 FLOPS = 2 * NQ * SLOTS * (D + DV)
@@ -36,6 +37,7 @@ def tile_attend_pkv4_soft_kb_gate_kernel(tc, qT, k_words, k_scales, v_words, v_s
     with ExitStack() as ctx:
         keep = ctx.enter_context(tc.tile_pool(name="keep", bufs=1))
         windows = ctx.enter_context(tc.tile_pool(name="windows", bufs=1))
+        late = ctx.enter_context(tc.tile_pool(name="late", bufs=1))
         psum = ctx.enter_context(tc.psum_pool(name="psum", bufs=1))
 
         def sbuf(name, shape, dtype, tag=None):
@@ -66,6 +68,8 @@ def tile_attend_pkv4_soft_kb_gate_kernel(tc, qT, k_words, k_scales, v_words, v_s
             scale_rows[QUADRANT - SCALE_ROWS :, :].unsqueeze(0).to_broadcast([QUADRANT // SCALE_ROWS, SCALE_ROWS, TOKENS // 4]),
         )
         nc.sync.dma_start(offsets[:], offs)
+        og_sb = sbuf("og_sb", [P, DV], F32)
+        nc.sync.dma_start(og_sb[:], og[0])
         nc.sync.dma_start(v_offsets[:], voffs)
         nc.sync.dma_start(
             q_raw[:].rearrange("p o j w -> p o (j w)"),
@@ -78,20 +82,11 @@ def tile_attend_pkv4_soft_kb_gate_kernel(tc, qT, k_words, k_scales, v_words, v_s
             nc.vector.memset(ks_pool[quadrant(quad), :].bitcast(I32), 0)
         nc.vector.memset(k_planes[:].bitcast(I32), 0)
 
-        og_sb = sbuf("og_sb", [P, DV], F32)
-        nc.gpsimd.dma_start(og_sb[:], og[0])
         half_tanh = sbuf("half_tanh", [P, DV], F32)
         gate = sbuf("gate", [P, DV], F32)
         nc.scalar.activation(half_tanh[:], og_sb[:], ACT.Tanh, scale=0.5)
         nc.scalar.activation(gate[:], half_tanh[:], ACT.Copy, scale=0.5, bias=0.5)
 
-        vsc_pool = sbuf("vsc_pool", [P, POOL_PAGES * DV], U8)
-        nc.gpsimd.memset(vsc_pool[:].bitcast(I32), 0)
-        for quad in range(QUADRANTS):
-            nc.gpsimd.dma_start(
-                vsc_pool[quadrant(quad, SCALE_ROWS), :].bitcast(I32).rearrange("f (u e) -> f u e", u=POOL_PAGES),
-                v_scales[:, SCALE_ROWS * quad : SCALE_ROWS * (quad + 1), :].bitcast(I32).rearrange("u f e -> f u e"),
-            )
         identity = sbuf("identity", [P, P], F32)
         make_identity(nc, identity[:])
 
@@ -100,7 +95,7 @@ def tile_attend_pkv4_soft_kb_gate_kernel(tc, qT, k_words, k_scales, v_words, v_s
         q_scales = sbuf("q_scales", [P, D_PASSES * NQ], U8)
         nc.scalar.copy(q_grouped[:], q_raw[:].rearrange("p o j w -> p o w j"))
 
-        ks_rows = sbuf("ks_rows", [P, SLOTS], U8, "rows_then_v")
+        ks_rows = late.tile([P, SLOTS], U8, name="ks_rows", offset=0, align_bytes=64)
         nc.vector.tensor_copy(ks_rows[:], ks_pool[:].indirect(offsets[:]))
         in_place = ((0, 0), (D_PASSES - 1, QUADRANTS - 1))
         for o in range(D_PASSES):
@@ -116,17 +111,22 @@ def tile_attend_pkv4_soft_kb_gate_kernel(tc, qT, k_words, k_scales, v_words, v_s
         nc.sync.dma_start(kb_pool[:], kb)
         vs_pool = windows.tile([P, TOKENS], F32, name="vs_pool", offset=row_bytes)
         nc.sync.dma_start(vs_pool[:], vs)
-        v_pool = sbuf("v_pool", [P, POOL_PAGES * DV], U32, "rows_then_v")
+        v_pool = late.tile([P, POOL_PAGES * DV], U32, name="v_pool", offset=LATE_BORDER, align_bytes=64)
         nc.sync.dma_start(
             v_pool[:].bitcast(I32).rearrange("p (u e) -> p u e", u=POOL_PAGES),
             v_words.rearrange("u p e r -> p u (e r)").bitcast(I32),
         )
+        vsc_pool = late.tile([P, POOL_PAGES * DV], U8, name="vsc_pool", offset=0, align_bytes=64)
+        nc.gpsimd.memset(vsc_pool[:].bitcast(I32), 0)
+        for quad in range(QUADRANTS):
+            nc.sync.dma_start(
+                vsc_pool[quadrant(quad, SCALE_ROWS), :].bitcast(I32).rearrange("f (u e) -> f u e", u=POOL_PAGES),
+                v_scales[:, SCALE_ROWS * quad : SCALE_ROWS * (quad + 1), :].bitcast(I32).rearrange("u f e -> f u e"),
+            )
 
         nc.vector.quantize_mx(
             out=q_codes[:].bitcast(FP8X4), scales=q_scales[:], in_=q_grouped[:].rearrange("p o w j -> p (o w j)")
         )
-        v_plane = sbuf("v_plane", [P, PAGES * DV], U8)
-        nc.vector.tensor_copy(v_plane[:], vsc_pool[:].indirect(v_offsets[:]))
 
         k_pairs = [sbuf("k_pairs%d" % g, [P, PAGE], U32) for g in range(PAGES)]
         k_parted = [sbuf("k_parted%d" % g, [P, D_PASSES, FP4_WORD_BYTES * PAGE], U8) for g in range(PAGES)]
@@ -232,6 +232,8 @@ def tile_attend_pkv4_soft_kb_gate_kernel(tc, qT, k_words, k_scales, v_words, v_s
             empty_bank(g)
         v_codes = sbuf("v_codes", [P, PAGES * DV], U32)
         nc.vector.tensor_copy(v_codes[:], v_pool[:].indirect(v_offsets[:]))
+        v_plane = sbuf("v_plane", [P, PAGES * DV], U8)
+        nc.vector.tensor_copy(v_plane[:], vsc_pool[:].indirect(v_offsets[:]))
         nc.vector.reciprocal(inv_total[:], total[:])
         for g in range(PAGES):
             quantise(g)

@@ -36,7 +36,6 @@ def tile_attend_pkv4_soft_kb_gate_kernel(tc, qT, k_words, k_scales, v_words, v_s
     nc = tc.nc
     with ExitStack() as ctx:
         keep = ctx.enter_context(tc.tile_pool(name="keep", bufs=1))
-        windows = ctx.enter_context(tc.tile_pool(name="windows", bufs=1))
         late = ctx.enter_context(tc.tile_pool(name="late", bufs=1))
         psum = ctx.enter_context(tc.psum_pool(name="psum", bufs=1))
 
@@ -57,29 +56,25 @@ def tile_attend_pkv4_soft_kb_gate_kernel(tc, qT, k_words, k_scales, v_words, v_s
         def quadrant(quad, rows=QUADRANT):
             return slice(QUADRANT * quad, QUADRANT * quad + rows)
 
-        row_bytes = 4 * TOKENS
-        ks_pool = windows.tile([P, TOKENS], U8, name="ks_pool", offset=row_bytes - TOKENS // 2)
+        ks_pool = sbuf("ks_pool", [P, TOKENS], U8, "ks_then_vs")
         k_pool = sbuf("k_pool", [P, TOKENS], U32)
         q_raw = sbuf("q_raw", [P, D_PASSES, PACK, NQ], F32)
-        scale_rows = k_scales.bitcast(I32).rearrange("o f t -> (o f) t")
-        nc.sync.dma_start(ks_pool[quadrant(0), :].bitcast(I32), scale_rows)
-        nc.sync.dma_start(
-            ks_pool[quadrant(QUADRANTS - 1), :].bitcast(I32),
-            scale_rows[QUADRANT - SCALE_ROWS :, :].unsqueeze(0).to_broadcast([QUADRANT // SCALE_ROWS, SCALE_ROWS, TOKENS // 4]),
-        )
-        nc.sync.dma_start(offsets[:], offs)
+        kb_columns = sbuf("kb_columns", [P, TOKENS // P], F32)
         og_sb = sbuf("og_sb", [P, DV], F32)
+        nc.sync.dma_start(ks_pool[quadrant(0), :].bitcast(I32), k_scales.bitcast(I32).rearrange("o f t -> (o f) t"))
+        nc.sync.dma_start(offsets[:], offs)
+        nc.sync.dma_start(kb_columns[:], kb[0].rearrange("(p c) -> p c", p=P))
         nc.sync.dma_start(og_sb[:], og[0])
         nc.sync.dma_start(v_offsets[:], voffs)
+        nc.sync.dma_start(k_pool[:].bitcast(I32), k_words[0].rearrange("p t b -> p (t b)").bitcast(I32))
         nc.sync.dma_start(
             q_raw[:].rearrange("p o j w -> p o (j w)"),
             qT[0].rearrange("(o p j) w -> p o (j w)", o=D_PASSES, j=PACK),
         )
-        nc.sync.dma_start(k_pool[:].bitcast(I32), k_words[0].rearrange("p t b -> p (t b)").bitcast(I32))
 
         k_planes = sbuf("k_planes", [P, D_PASSES * SLOTS], U8)
-        for quad in range(1, QUADRANTS - 1):
-            nc.vector.memset(ks_pool[quadrant(quad), :].bitcast(I32), 0)
+        nc.vector.memset(ks_pool[quadrant(1), :].bitcast(I32), 0)
+        nc.vector.memset(ks_pool[quadrant(2, 2 * QUADRANT), :].bitcast(I32), 0)
         nc.vector.memset(k_planes[:].bitcast(I32), 0)
 
         half_tanh = sbuf("half_tanh", [P, DV], F32)
@@ -90,14 +85,27 @@ def tile_attend_pkv4_soft_kb_gate_kernel(tc, qT, k_words, k_scales, v_words, v_s
         identity = sbuf("identity", [P, P], F32)
         make_identity(nc, identity[:])
 
-        q_grouped = sbuf("q_grouped", [P, D_PASSES, NQ, PACK], BF16)
+        q_grouped = sbuf("q_grouped", [P, D_PASSES, NQ, PACK], BF16, "q_then_pairs")
         q_codes = sbuf("q_codes", [P, D_PASSES * NQ], U32)
         q_scales = sbuf("q_scales", [P, D_PASSES * NQ], U8)
         nc.scalar.copy(q_grouped[:], q_raw[:].rearrange("p o j w -> p o w j"))
 
+        kb_pool = sbuf("kb_pool", [P, TOKENS], F32)
+        per_bank = PAGE // P
+        for b in range(TOKENS // PAGE):
+            spread = bank("spread%d" % b, [P, per_bank, P], "spread_bank%d" % (b % PAGES))
+            for c in range(per_bank):
+                column = b * per_bank + c
+                nc.tensor.transpose(spread[:, c, :], kb_columns[:, column : column + 1].to_broadcast([P, P]), identity[:])
+            nc.scalar.activation(
+                kb_pool[:].rearrange("q (p b c) -> q b p c", p=P, c=per_bank)[:, b],
+                spread[:].rearrange("q c p -> q p c"),
+                ACT.Copy,
+            )
+
         ks_rows = late.tile([P, SLOTS], U8, name="ks_rows", offset=0, align_bytes=64)
         nc.vector.tensor_copy(ks_rows[:], ks_pool[:].indirect(offsets[:]))
-        in_place = ((0, 0), (D_PASSES - 1, QUADRANTS - 1))
+        in_place = ((0, 0),)
         for o in range(D_PASSES):
             for quad in range(QUADRANTS):
                 target = k_planes[quadrant(quad, SCALE_ROWS), o * SLOTS : (o + 1) * SLOTS].bitcast(I32)
@@ -107,9 +115,7 @@ def tile_attend_pkv4_soft_kb_gate_kernel(tc, qT, k_words, k_scales, v_words, v_s
                     first = SCALE_ROWS * (QUADRANTS * o + quad)
                     nc.sync.dma_start(target, ks_rows[first : first + SCALE_ROWS, :].bitcast(I32))
 
-        kb_pool = windows.tile([P, TOKENS], F32, name="kb_pool", offset=0)
-        nc.sync.dma_start(kb_pool[:], kb)
-        vs_pool = windows.tile([P, TOKENS], F32, name="vs_pool", offset=row_bytes)
+        vs_pool = sbuf("vs_pool", [P, TOKENS], F32, "ks_then_vs")
         nc.sync.dma_start(vs_pool[:], vs)
         v_pool = late.tile([P, POOL_PAGES * DV], U32, name="v_pool", offset=LATE_BORDER, align_bytes=64)
         nc.sync.dma_start(
@@ -124,11 +130,8 @@ def tile_attend_pkv4_soft_kb_gate_kernel(tc, qT, k_words, k_scales, v_words, v_s
                 v_scales[:, SCALE_ROWS * quad : SCALE_ROWS * (quad + 1), :].bitcast(I32).rearrange("u f e -> f u e"),
             )
 
-        nc.vector.quantize_mx(
-            out=q_codes[:].bitcast(FP8X4), scales=q_scales[:], in_=q_grouped[:].rearrange("p o w j -> p (o w j)")
-        )
 
-        k_pairs = [sbuf("k_pairs%d" % g, [P, PAGE], U32) for g in range(PAGES)]
+        k_pairs = [sbuf("k_pairs%d" % g, [P, PAGE], U32, "q_then_pairs" if g == last else None) for g in range(PAGES)]
         k_parted = [sbuf("k_parted%d" % g, [P, D_PASSES, FP4_WORD_BYTES * PAGE], U8) for g in range(PAGES)]
 
         def gather_keys(g):
@@ -141,9 +144,14 @@ def tile_attend_pkv4_soft_kb_gate_kernel(tc, qT, k_words, k_scales, v_words, v_s
             )
 
         gather_keys(0)
-        for g in range(1, PAGES):
+        for g in range(1, last):
             gather_keys(g)
             part_keys(g - 1)
+        nc.vector.quantize_mx(
+            out=q_codes[:].bitcast(FP8X4), scales=q_scales[:], in_=q_grouped[:].rearrange("p o w j -> p (o w j)")
+        )
+        gather_keys(last)
+        part_keys(last - 1)
         part_keys(last)
 
         raw_scores = [sbuf("raw_scores%d" % g, [P, PAGE], F32) for g in range(PAGES)]

@@ -26,7 +26,6 @@ QUADRANTS, QUADRANT = 4, 32
 SCALE_ROWS = 4
 LIST_ROWS = 16
 HALVES = 2
-LATE_BORDER = POOL_PAGES * DV
 FP4_WORD_BYTES = 2
 
 FLOPS = 2 * NQ * SLOTS * (D + DV)
@@ -36,7 +35,7 @@ def tile_attend_pkv4_soft_kb_gate_kernel(tc, qT, k_words, k_scales, v_words, v_s
     nc = tc.nc
     with ExitStack() as ctx:
         keep = ctx.enter_context(tc.tile_pool(name="keep", bufs=1))
-        late = ctx.enter_context(tc.tile_pool(name="late", bufs=1))
+        held = ctx.enter_context(tc.tile_pool(name="held", bufs=1))
         psum = ctx.enter_context(tc.psum_pool(name="psum", bufs=1))
 
         def sbuf(name, shape, dtype, tag=None):
@@ -56,16 +55,20 @@ def tile_attend_pkv4_soft_kb_gate_kernel(tc, qT, k_words, k_scales, v_words, v_s
         def quadrant(quad, rows=QUADRANT):
             return slice(QUADRANT * quad, QUADRANT * quad + rows)
 
-        ks_pool = sbuf("ks_pool", [P, TOKENS], U8, "ks_then_vs")
+        ks_pool = held.tile([P, TOKENS], U8, name="ks_pool", offset=0)
         k_pool = sbuf("k_pool", [P, TOKENS], U32)
         q_raw = sbuf("q_raw", [P, D_PASSES, PACK, NQ], F32)
         kb_columns = sbuf("kb_columns", [P, TOKENS // P], F32)
-        og_sb = sbuf("og_sb", [P, DV], F32)
         nc.sync.dma_start(ks_pool[quadrant(0), :].bitcast(I32), k_scales.bitcast(I32).rearrange("o f t -> (o f) t"))
         nc.sync.dma_start(offsets[:], offs)
         nc.sync.dma_start(kb_columns[:], kb[0].rearrange("(p c) -> p c", p=P))
-        nc.sync.dma_start(og_sb[:], og[0])
         nc.sync.dma_start(v_offsets[:], voffs)
+        vsc_pool = sbuf("vsc_pool", [P, POOL_PAGES * DV], U8)
+        nc.gpsimd.memset(vsc_pool[:].bitcast(I32), 0)
+        nc.sync.dma_start(
+            vsc_pool[: QUADRANTS * SCALE_ROWS, :].bitcast(I32).rearrange("f (u e) -> f u e", u=POOL_PAGES),
+            v_scales.bitcast(I32).rearrange("u f e -> f u e"),
+        )
         nc.sync.dma_start(k_pool[:].bitcast(I32), k_words[0].rearrange("p t b -> p (t b)").bitcast(I32))
         nc.sync.dma_start(
             q_raw[:].rearrange("p o j w -> p o (j w)"),
@@ -77,18 +80,17 @@ def tile_attend_pkv4_soft_kb_gate_kernel(tc, qT, k_words, k_scales, v_words, v_s
         nc.vector.memset(ks_pool[quadrant(2, 2 * QUADRANT), :].bitcast(I32), 0)
         nc.vector.memset(k_planes[:].bitcast(I32), 0)
 
-        half_tanh = sbuf("half_tanh", [P, DV], F32)
-        gate = sbuf("gate", [P, DV], F32)
-        nc.scalar.activation(half_tanh[:], og_sb[:], ACT.Tanh, scale=0.5)
-        nc.scalar.activation(gate[:], half_tanh[:], ACT.Copy, scale=0.5, bias=0.5)
 
         identity = sbuf("identity", [P, P], F32)
         make_identity(nc, identity[:])
 
-        q_grouped = sbuf("q_grouped", [P, D_PASSES, NQ, PACK], BF16, "q_then_pairs")
-        q_codes = sbuf("q_codes", [P, D_PASSES * NQ], U32)
-        q_scales = sbuf("q_scales", [P, D_PASSES * NQ], U8)
-        nc.scalar.copy(q_grouped[:], q_raw[:].rearrange("p o j w -> p o w j"))
+        q_grouped = [sbuf("q_grouped%d" % o, [P, NQ, PACK], BF16, "q_then_pairs" if o == 0 else None) for o in range(D_PASSES)]
+        q_codes = [sbuf("q_codes%d" % o, [P, NQ], U32) for o in range(D_PASSES)]
+        q_scales = [sbuf("q_scales%d" % o, [P, NQ], U8) for o in range(D_PASSES)]
+        for o in reversed(range(D_PASSES)):
+            nc.scalar.copy(
+                q_grouped[o][:].rearrange("p (c i) j -> p c j i", i=PACK), q_raw[:, o].rearrange("p j (c i) -> p c j i", i=PACK)
+            )
 
         kb_pool = sbuf("kb_pool", [P, TOKENS], F32)
         per_bank = PAGE // P
@@ -103,7 +105,7 @@ def tile_attend_pkv4_soft_kb_gate_kernel(tc, qT, k_words, k_scales, v_words, v_s
                 ACT.Copy,
             )
 
-        ks_rows = late.tile([P, SLOTS], U8, name="ks_rows", offset=0, align_bytes=64)
+        ks_rows = sbuf("ks_rows", [P, SLOTS], U8, "rows_then_v")
         nc.vector.tensor_copy(ks_rows[:], ks_pool[:].indirect(offsets[:]))
         in_place = ((0, 0),)
         for o in range(D_PASSES):
@@ -115,20 +117,28 @@ def tile_attend_pkv4_soft_kb_gate_kernel(tc, qT, k_words, k_scales, v_words, v_s
                     first = SCALE_ROWS * (QUADRANTS * o + quad)
                     nc.sync.dma_start(target, ks_rows[first : first + SCALE_ROWS, :].bitcast(I32))
 
-        vs_pool = sbuf("vs_pool", [P, TOKENS], F32, "ks_then_vs")
+        og_sb = held.tile([P, DV], F32, name="og_sb", offset=0)
+        nc.sync.dma_start(og_sb[:], og[0])
+        half_tanh = sbuf("half_tanh", [P, DV], F32)
+        gate = sbuf("gate", [P, DV], F32)
+        nc.scalar.activation(half_tanh[:], og_sb[:], ACT.Tanh, scale=0.5)
+        nc.scalar.activation(gate[:], half_tanh[:], ACT.Copy, scale=0.5, bias=0.5)
+        vs_pool = held.tile([P, TOKENS], F32, name="vs_pool", offset=4 * DV)
         nc.sync.dma_start(vs_pool[:], vs)
-        v_pool = late.tile([P, POOL_PAGES * DV], U32, name="v_pool", offset=LATE_BORDER, align_bytes=64)
+        vsc_rows = sbuf("vsc_rows", [P, PAGES * DV], U8)
+        v_plane = sbuf("v_plane", [P, PAGES * DV], U8)
+        nc.gpsimd.memset(v_plane[:].bitcast(I32), 0)
+        nc.vector.tensor_copy(vsc_rows[:], vsc_pool[:].indirect(v_offsets[:]))
+        for quad in range(QUADRANTS):
+            nc.sync.dma_start(
+                v_plane[quadrant(quad, SCALE_ROWS), :].bitcast(I32),
+                vsc_rows[SCALE_ROWS * quad : SCALE_ROWS * (quad + 1), :].bitcast(I32),
+            )
+        v_pool = sbuf("v_pool", [P, POOL_PAGES * DV], U32, "rows_then_v")
         nc.sync.dma_start(
             v_pool[:].bitcast(I32).rearrange("p (u e) -> p u e", u=POOL_PAGES),
             v_words.rearrange("u p e r -> p u (e r)").bitcast(I32),
         )
-        vsc_pool = late.tile([P, POOL_PAGES * DV], U8, name="vsc_pool", offset=0, align_bytes=64)
-        nc.gpsimd.memset(vsc_pool[:].bitcast(I32), 0)
-        for quad in range(QUADRANTS):
-            nc.sync.dma_start(
-                vsc_pool[quadrant(quad, SCALE_ROWS), :].bitcast(I32).rearrange("f (u e) -> f u e", u=POOL_PAGES),
-                v_scales[:, SCALE_ROWS * quad : SCALE_ROWS * (quad + 1), :].bitcast(I32).rearrange("u f e -> f u e"),
-            )
 
 
         k_pairs = [sbuf("k_pairs%d" % g, [P, PAGE], U32, "q_then_pairs" if g == last else None) for g in range(PAGES)]
@@ -143,13 +153,18 @@ def tile_attend_pkv4_soft_kb_gate_kernel(tc, qT, k_words, k_scales, v_words, v_s
                 k_pairs[g][:].bitcast(U16).rearrange("p (s o) -> p o s", o=D_PASSES),
             )
 
+        def quantise_queries(o):
+            nc.vector.quantize_mx(
+                out=q_codes[o][:].bitcast(FP8X4), scales=q_scales[o][:], in_=q_grouped[o][:].rearrange("p w j -> p (w j)")
+            )
+
         gather_keys(0)
-        for g in range(1, last):
-            gather_keys(g)
-            part_keys(g - 1)
-        nc.vector.quantize_mx(
-            out=q_codes[:].bitcast(FP8X4), scales=q_scales[:], in_=q_grouped[:].rearrange("p o w j -> p (o w j)")
-        )
+        gather_keys(1)
+        part_keys(0)
+        gather_keys(2)
+        quantise_queries(1)
+        part_keys(1)
+        quantise_queries(0)
         gather_keys(last)
         part_keys(last - 1)
         part_keys(last)
@@ -160,8 +175,8 @@ def tile_attend_pkv4_soft_kb_gate_kernel(tc, qT, k_words, k_scales, v_words, v_s
             for o in reversed(range(D_PASSES)):
                 nc.tensor.matmul_mx(
                     out=score_bank[:],
-                    lhsT=q_codes[:, o * NQ : (o + 1) * NQ].bitcast(FP8X4),
-                    lhsT_scale=q_scales[:, o * NQ : (o + 1) * NQ],
+                    lhsT=q_codes[o][:].bitcast(FP8X4),
+                    lhsT_scale=q_scales[o][:],
                     rhs=k_parted[g][:, o, :].bitcast(FP4X4),
                     rhs_scale=k_planes[:, o * SLOTS + g * PAGE : o * SLOTS + (g + 1) * PAGE],
                     start=(o == D_PASSES - 1),
@@ -240,8 +255,6 @@ def tile_attend_pkv4_soft_kb_gate_kernel(tc, qT, k_words, k_scales, v_words, v_s
             empty_bank(g)
         v_codes = sbuf("v_codes", [P, PAGES * DV], U32)
         nc.vector.tensor_copy(v_codes[:], v_pool[:].indirect(v_offsets[:]))
-        v_plane = sbuf("v_plane", [P, PAGES * DV], U8)
-        nc.vector.tensor_copy(v_plane[:], vsc_pool[:].indirect(v_offsets[:]))
         nc.vector.reciprocal(inv_total[:], total[:])
         for g in range(PAGES):
             quantise(g)

@@ -35,7 +35,6 @@ def tile_attend_pkv4_soft_kb_gate_kernel(tc, qT, k_words, k_scales, v_words, v_s
     nc = tc.nc
     with ExitStack() as ctx:
         keep = ctx.enter_context(tc.tile_pool(name="keep", bufs=1))
-        held = ctx.enter_context(tc.tile_pool(name="held", bufs=1))
         psum = ctx.enter_context(tc.psum_pool(name="psum", bufs=1))
 
         def sbuf(name, shape, dtype, tag=None):
@@ -55,13 +54,15 @@ def tile_attend_pkv4_soft_kb_gate_kernel(tc, qT, k_words, k_scales, v_words, v_s
         def quadrant(quad, rows=QUADRANT):
             return slice(QUADRANT * quad, QUADRANT * quad + rows)
 
-        ks_pool = held.tile([P, TOKENS], U8, name="ks_pool", offset=0)
+        ks_pool = sbuf("ks_pool", [P, TOKENS], U8, "ks_then_vs")
         k_pool = sbuf("k_pool", [P, TOKENS], U32)
         q_raw = sbuf("q_raw", [P, D_PASSES, PACK, NQ], F32)
         kb_columns = sbuf("kb_columns", [P, TOKENS // P], F32)
         nc.sync.dma_start(ks_pool[quadrant(0), :].bitcast(I32), k_scales.bitcast(I32).rearrange("o f t -> (o f) t"))
         nc.sync.dma_start(offsets[:], offs)
         nc.sync.dma_start(kb_columns[:], kb[0].rearrange("(p c) -> p c", p=P))
+        og_sb = sbuf("og_sb", [P, DV], F32)
+        nc.sync.dma_start(og_sb[:], og[0])
         nc.sync.dma_start(v_offsets[:], voffs)
         vsc_pool = sbuf("vsc_pool", [P, POOL_PAGES * DV], U8)
         nc.gpsimd.memset(vsc_pool[:].bitcast(I32), 0)
@@ -81,6 +82,11 @@ def tile_attend_pkv4_soft_kb_gate_kernel(tc, qT, k_words, k_scales, v_words, v_s
         nc.vector.memset(k_planes[:].bitcast(I32), 0)
 
 
+        half_tanh = sbuf("half_tanh", [P, DV], F32)
+        gate = sbuf("gate", [P, DV], F32)
+        nc.scalar.activation(half_tanh[:], og_sb[:], ACT.Tanh, scale=0.5)
+        nc.scalar.activation(gate[:], half_tanh[:], ACT.Copy, scale=0.5, bias=0.5)
+
         identity = sbuf("identity", [P, P], F32)
         make_identity(nc, identity[:])
 
@@ -88,9 +94,7 @@ def tile_attend_pkv4_soft_kb_gate_kernel(tc, qT, k_words, k_scales, v_words, v_s
         q_codes = [sbuf("q_codes%d" % o, [P, NQ], U32) for o in range(D_PASSES)]
         q_scales = [sbuf("q_scales%d" % o, [P, NQ], U8) for o in range(D_PASSES)]
         for o in reversed(range(D_PASSES)):
-            nc.scalar.copy(
-                q_grouped[o][:].rearrange("p (c i) j -> p c j i", i=PACK), q_raw[:, o].rearrange("p j (c i) -> p c j i", i=PACK)
-            )
+            nc.scalar.copy(q_grouped[o][:], q_raw[:, o].rearrange("p j w -> p w j"))
 
         kb_pool = sbuf("kb_pool", [P, TOKENS], F32)
         per_bank = PAGE // P
@@ -117,13 +121,7 @@ def tile_attend_pkv4_soft_kb_gate_kernel(tc, qT, k_words, k_scales, v_words, v_s
                     first = SCALE_ROWS * (QUADRANTS * o + quad)
                     nc.sync.dma_start(target, ks_rows[first : first + SCALE_ROWS, :].bitcast(I32))
 
-        og_sb = held.tile([P, DV], F32, name="og_sb", offset=0)
-        nc.sync.dma_start(og_sb[:], og[0])
-        half_tanh = sbuf("half_tanh", [P, DV], F32)
-        gate = sbuf("gate", [P, DV], F32)
-        nc.scalar.activation(half_tanh[:], og_sb[:], ACT.Tanh, scale=0.5)
-        nc.scalar.activation(gate[:], half_tanh[:], ACT.Copy, scale=0.5, bias=0.5)
-        vs_pool = held.tile([P, TOKENS], F32, name="vs_pool", offset=4 * DV)
+        vs_pool = sbuf("vs_pool", [P, TOKENS], F32, "ks_then_vs")
         nc.sync.dma_start(vs_pool[:], vs)
         vsc_rows = sbuf("vsc_rows", [P, PAGES * DV], U8)
         v_plane = sbuf("v_plane", [P, PAGES * DV], U8)

@@ -35,13 +35,17 @@ def tile_attend_pkv4_soft_kb_gate_kernel(tc, qT, k_words, k_scales, v_words, v_s
     nc = tc.nc
     with ExitStack() as ctx:
         keep = ctx.enter_context(tc.tile_pool(name="keep", bufs=1))
+        late = ctx.enter_context(tc.tile_pool(name="late", bufs=1))
         psum = ctx.enter_context(tc.psum_pool(name="psum", bufs=1))
 
         def sbuf(name, shape, dtype, tag=None):
             return keep.tile(shape, dtype, name=name, tag=tag or name, align_bytes=64)
 
-        def bank(name, shape, tag=None):
-            return psum.tile(shape, F32, name=name, tag=tag or name)
+        def bank(name, shape, tag):
+            return psum.tile(shape, F32, name=name, tag=tag)
+
+        def quadrant(quad, rows=QUADRANT):
+            return slice(QUADRANT * quad, QUADRANT * quad + rows)
 
         offsets = keep.tile([P, SLOTS // LIST_ROWS], U16, name="offsets")
         v_offsets = keep.tile([P, PAGES * DV // LIST_ROWS], U16, name="v_offsets")
@@ -51,21 +55,21 @@ def tile_attend_pkv4_soft_kb_gate_kernel(tc, qT, k_words, k_scales, v_words, v_s
         def page_offsets(g):
             return offsets[:, g * cols : (g + 1) * cols]
 
-        def quadrant(quad, rows=QUADRANT):
-            return slice(QUADRANT * quad, QUADRANT * quad + rows)
+        half_window = TOKENS // 2
+        ks_pool = late.tile([P, TOKENS], U8, name="ks_pool", offset=half_window)
+        v_pool = late.tile([P, POOL_PAGES * DV], U32, name="v_pool", offset=0)
+        vs_pool = late.tile([P, TOKENS], F32, name="vs_pool", offset=TOKENS)
 
-        ks_pool = sbuf("ks_pool", [P, TOKENS], U8, "ks_then_vs")
         k_pool = sbuf("k_pool", [P, TOKENS], U32)
-        q_raw = sbuf("q_raw", [P, D_PASSES, PACK, NQ], F32)
+        q_raw = sbuf("q_raw", [P, D_PASSES, PACK, NQ], F32, "q_then_kb")
         kb_columns = sbuf("kb_columns", [P, TOKENS // P], F32)
+        vsc_pool = sbuf("vsc_pool", [P, POOL_PAGES * DV], U8)
+        og_sb = sbuf("og_sb", [P, DV], F32)
+        nc.vector.memset(vsc_pool[:].bitcast(I32), 0)
         nc.sync.dma_start(ks_pool[quadrant(0), :].bitcast(I32), k_scales.bitcast(I32).rearrange("o f t -> (o f) t"))
         nc.sync.dma_start(offsets[:], offs)
         nc.sync.dma_start(kb_columns[:], kb[0].rearrange("(p c) -> p c", p=P))
-        og_sb = sbuf("og_sb", [P, DV], F32)
-        nc.sync.dma_start(og_sb[:], og[0])
         nc.sync.dma_start(v_offsets[:], voffs)
-        vsc_pool = sbuf("vsc_pool", [P, POOL_PAGES * DV], U8)
-        nc.gpsimd.memset(vsc_pool[:].bitcast(I32), 0)
         nc.sync.dma_start(
             vsc_pool[: QUADRANTS * SCALE_ROWS, :].bitcast(I32).rearrange("f (u e) -> f u e", u=POOL_PAGES),
             v_scales.bitcast(I32).rearrange("u f e -> f u e"),
@@ -75,26 +79,17 @@ def tile_attend_pkv4_soft_kb_gate_kernel(tc, qT, k_words, k_scales, v_words, v_s
             q_raw[:].rearrange("p o j w -> p o (j w)"),
             qT[0].rearrange("(o p j) w -> p o (j w)", o=D_PASSES, j=PACK),
         )
+        nc.sync.dma_start(og_sb[:], og[0])
 
         k_planes = sbuf("k_planes", [P, D_PASSES * SLOTS], U8)
+        v_plane = sbuf("v_plane", [P, PAGES * DV], U8)
         nc.vector.memset(ks_pool[quadrant(1), :].bitcast(I32), 0)
         nc.vector.memset(ks_pool[quadrant(2, 2 * QUADRANT), :].bitcast(I32), 0)
         nc.vector.memset(k_planes[:].bitcast(I32), 0)
-
-
-        half_tanh = sbuf("half_tanh", [P, DV], F32)
-        gate = sbuf("gate", [P, DV], F32)
-        nc.scalar.activation(half_tanh[:], og_sb[:], ACT.Tanh, scale=0.5)
-        nc.scalar.activation(gate[:], half_tanh[:], ACT.Copy, scale=0.5, bias=0.5)
+        nc.vector.memset(v_plane[:].bitcast(I32), 0)
 
         identity = sbuf("identity", [P, P], F32)
         make_identity(nc, identity[:])
-
-        q_grouped = [sbuf("q_grouped%d" % o, [P, NQ, PACK], BF16, "q_then_pairs" if o == 0 else None) for o in range(D_PASSES)]
-        q_codes = [sbuf("q_codes%d" % o, [P, NQ], U32) for o in range(D_PASSES)]
-        q_scales = [sbuf("q_scales%d" % o, [P, NQ], U8) for o in range(D_PASSES)]
-        for o in reversed(range(D_PASSES)):
-            nc.scalar.copy(q_grouped[o][:], q_raw[:, o].rearrange("p j w -> p w j"))
 
         kb_pool = sbuf("kb_pool", [P, TOKENS], F32)
         per_bank = PAGE // P
@@ -109,35 +104,44 @@ def tile_attend_pkv4_soft_kb_gate_kernel(tc, qT, k_words, k_scales, v_words, v_s
                 ACT.Copy,
             )
 
-        ks_rows = sbuf("ks_rows", [P, SLOTS], U8, "rows_then_v")
+        q_grouped = [sbuf("q_grouped%d" % o, [P, NQ, PACK], BF16, "q_then_pairs" if o == 0 else None) for o in range(D_PASSES)]
+        q_codes = [sbuf("q_codes%d" % o, [P, NQ], U32) for o in range(D_PASSES)]
+        q_scales = [sbuf("q_scales%d" % o, [P, NQ], U8) for o in range(D_PASSES)]
+        for o in reversed(range(D_PASSES)):
+            nc.scalar.copy(q_grouped[o][:], q_raw[:, o].rearrange("p j w -> p w j"))
+
+        biases = sbuf("biases", [P, SLOTS], F32, "q_then_kb")
+        for g in range(PAGES):
+            nc.scalar.activation(biases[:, g * PAGE : (g + 1) * PAGE], kb_pool[:].indirect(page_offsets(g)), ACT.Copy)
+
+        half_tanh = sbuf("half_tanh", [P, DV], F32)
+        gate = sbuf("gate", [P, DV], F32)
+        nc.scalar.activation(half_tanh[:], og_sb[:], ACT.Tanh, scale=0.5)
+        nc.scalar.activation(gate[:], half_tanh[:], ACT.Copy, scale=0.5, bias=0.5)
+
+        ks_rows = sbuf("ks_rows", [P, SLOTS], U8)
         nc.vector.tensor_copy(ks_rows[:], ks_pool[:].indirect(offsets[:]))
-        in_place = ((0, 0),)
-        for o in range(D_PASSES):
+        for o in reversed(range(D_PASSES)):
             for quad in range(QUADRANTS):
                 target = k_planes[quadrant(quad, SCALE_ROWS), o * SLOTS : (o + 1) * SLOTS].bitcast(I32)
-                if (o, quad) in in_place:
+                first = SCALE_ROWS * (QUADRANTS * o + quad)
+                if first == QUADRANT * quad:
                     nc.vector.tensor_copy(target, ks_rows[quadrant(quad, SCALE_ROWS), :].bitcast(I32))
                 else:
-                    first = SCALE_ROWS * (QUADRANTS * o + quad)
                     nc.sync.dma_start(target, ks_rows[first : first + SCALE_ROWS, :].bitcast(I32))
 
-        vs_pool = sbuf("vs_pool", [P, TOKENS], F32, "ks_then_vs")
+        nc.sync.dma_start(
+            v_pool[:].bitcast(I32).rearrange("p (u e) -> p u e", u=POOL_PAGES),
+            v_words.rearrange("u p e r -> p u (e r)").bitcast(I32),
+        )
         nc.sync.dma_start(vs_pool[:], vs)
         vsc_rows = sbuf("vsc_rows", [P, PAGES * DV], U8)
-        v_plane = sbuf("v_plane", [P, PAGES * DV], U8)
-        nc.gpsimd.memset(v_plane[:].bitcast(I32), 0)
         nc.vector.tensor_copy(vsc_rows[:], vsc_pool[:].indirect(v_offsets[:]))
         for quad in range(QUADRANTS):
             nc.sync.dma_start(
                 v_plane[quadrant(quad, SCALE_ROWS), :].bitcast(I32),
                 vsc_rows[SCALE_ROWS * quad : SCALE_ROWS * (quad + 1), :].bitcast(I32),
             )
-        v_pool = sbuf("v_pool", [P, POOL_PAGES * DV], U32, "rows_then_v")
-        nc.sync.dma_start(
-            v_pool[:].bitcast(I32).rearrange("p (u e) -> p u e", u=POOL_PAGES),
-            v_words.rearrange("u p e r -> p u (e r)").bitcast(I32),
-        )
-
 
         k_pairs = [sbuf("k_pairs%d" % g, [P, PAGE], U32, "q_then_pairs" if g == last else None) for g in range(PAGES)]
         k_parted = [sbuf("k_parted%d" % g, [P, D_PASSES, FP4_WORD_BYTES * PAGE], U8) for g in range(PAGES)]
@@ -167,7 +171,11 @@ def tile_attend_pkv4_soft_kb_gate_kernel(tc, qT, k_words, k_scales, v_words, v_s
         part_keys(last - 1)
         part_keys(last)
 
-        raw_scores = [sbuf("raw_scores%d" % g, [P, PAGE], F32) for g in range(PAGES)]
+        scores = [sbuf("scores%d" % g, [P, PAGE], F32) for g in range(PAGES)]
+        probs = [sbuf("probs%d" % g, [P, PAGE], F32) for g in range(PAGES)]
+        neg_page_max = sbuf("neg_page_max", [P, PAGES], F32)
+        page_sum = sbuf("page_sum", [P, PAGES], F32)
+        score_banks = []
         for g in range(PAGES):
             score_bank = bank("score_bank%d" % g, [P, PAGE], "bank%d" % g)
             for o in reversed(range(D_PASSES)):
@@ -180,15 +188,10 @@ def tile_attend_pkv4_soft_kb_gate_kernel(tc, qT, k_words, k_scales, v_words, v_s
                     start=(o == D_PASSES - 1),
                     stop=(o == 0),
                 )
-            nc.scalar.copy(raw_scores[g][:], score_bank[:])
-
-        scores = [sbuf("scores%d" % g, [P, PAGE], F32) for g in range(PAGES)]
-        probs = [sbuf("probs%d" % g, [P, PAGE], F32) for g in range(PAGES)]
-        neg_page_max = sbuf("neg_page_max", [P, PAGES], F32)
-        page_sum = sbuf("page_sum", [P, PAGES], F32)
+            score_banks.append(score_bank)
 
         def add_bias(g):
-            nc.vector.tensor_tensor(scores[g][:], kb_pool[:].indirect(page_offsets(g)), raw_scores[g][:], ALU.add)
+            nc.vector.tensor_tensor(scores[g][:], score_banks[g][:], biases[:, g * PAGE : (g + 1) * PAGE], ALU.add)
 
         def page_softmax(g):
             nc.vector.tensor_reduce(neg_page_max[:, g : g + 1], scores[g][:], AXIS_X, ALU.max, negate=True)
@@ -202,7 +205,7 @@ def tile_attend_pkv4_soft_kb_gate_kernel(tc, qT, k_words, k_scales, v_words, v_s
             page_softmax(g - 1)
         page_softmax(last)
 
-        scaled = [sbuf("scaled%d" % g, [P, PAGE], F32) for g in range(PAGES)]
+        scaled = [sbuf("scaled%d" % g, [P, PAGE], F32, "scaled_then_v" if g == last else None) for g in range(PAGES)]
         dealt = [sbuf("dealt%d" % g, [P, HALVES, P, HALVES], BF16) for g in range(PAGES)]
         weights = [sbuf("weights%d" % g, [P, NQ, PACK], BF16) for g in range(PAGES)]
         w_codes = [sbuf("w_codes%d" % g, [P, NQ], U32) for g in range(PAGES)]
@@ -251,7 +254,7 @@ def tile_attend_pkv4_soft_kb_gate_kernel(tc, qT, k_words, k_scales, v_words, v_s
         weigh(last)
         for g in range(PAGES):
             empty_bank(g)
-        v_codes = sbuf("v_codes", [P, PAGES * DV], U32)
+        v_codes = sbuf("v_codes", [P, PAGES * DV], U32, "scaled_then_v")
         nc.vector.tensor_copy(v_codes[:], v_pool[:].indirect(v_offsets[:]))
         nc.vector.reciprocal(inv_total[:], total[:])
         for g in range(PAGES):

@@ -130,11 +130,11 @@ def tile_attend_pkv4_soft_kb_gate_kernel(tc, qT, k_words, k_scales, v_words, v_s
                 else:
                     nc.sync.dma_start(target, ks_rows[first : first + SCALE_ROWS, :].bitcast(I32))
 
+        nc.sync.dma_start(vs_pool[:], vs)
         nc.sync.dma_start(
             v_pool[:].bitcast(I32).rearrange("p (u e) -> p u e", u=POOL_PAGES),
             v_words.rearrange("u p e r -> p u (e r)").bitcast(I32),
         )
-        nc.sync.dma_start(vs_pool[:], vs)
         vsc_rows = sbuf("vsc_rows", [P, PAGES * DV], U8)
         nc.vector.tensor_copy(vsc_rows[:], vsc_pool[:].indirect(v_offsets[:]))
         for quad in range(QUADRANTS):
@@ -172,7 +172,7 @@ def tile_attend_pkv4_soft_kb_gate_kernel(tc, qT, k_words, k_scales, v_words, v_s
         part_keys(last)
 
         scores = [sbuf("scores%d" % g, [P, PAGE], F32) for g in range(PAGES)]
-        probs = [sbuf("probs%d" % g, [P, PAGE], F32) for g in range(PAGES)]
+        probs = [sbuf("probs%d" % g, [P, PAGE], F32, "probs_then_sum" if g == last else None) for g in range(PAGES)]
         neg_page_max = sbuf("neg_page_max", [P, PAGES], F32)
         page_sum = sbuf("page_sum", [P, PAGES], F32)
         score_banks = []
@@ -199,13 +199,22 @@ def tile_attend_pkv4_soft_kb_gate_kernel(tc, qT, k_words, k_scales, v_words, v_s
                 probs[g][:], scores[g][:], ACT.Exp, bias=neg_page_max[:, g : g + 1], accum_out=page_sum[:, g : g + 1]
             )
 
-        add_bias(0)
-        for g in range(1, PAGES):
+        aside = last - 1
+        raw_scores = sbuf("raw_scores", [P, PAGE], F32, "raw_then_scaled")
+        nc.scalar.copy(raw_scores[:], score_banks[aside][:])
+        nc.gpsimd.tensor_tensor(scores[aside][:], raw_scores[:], biases[:, aside * PAGE : (aside + 1) * PAGE], ALU.add)
+        order = [g for g in range(PAGES) if g != aside] + [aside]
+        add_bias(order[0])
+        for earlier, g in zip(order, order[1:-1]):
             add_bias(g)
-            page_softmax(g - 1)
-        page_softmax(last)
+            page_softmax(earlier)
+        for g in order[-2:]:
+            page_softmax(g)
+        final = order[-1]
 
-        scaled = [sbuf("scaled%d" % g, [P, PAGE], F32, "scaled_then_v" if g == last else None) for g in range(PAGES)]
+        scaled_early = sbuf("scaled_early", [P, PAGES - 1, PAGE], F32, "raw_then_scaled")
+        scaled = {g: scaled_early[:, place] for place, g in enumerate(order[:-1])}
+        scaled[final] = sbuf("scaled_final", [P, PAGE], F32, "scaled_then_v")[:]
         dealt = [sbuf("dealt%d" % g, [P, HALVES, P, HALVES], BF16) for g in range(PAGES)]
         weights = [sbuf("weights%d" % g, [P, NQ, PACK], BF16) for g in range(PAGES)]
         w_codes = [sbuf("w_codes%d" % g, [P, NQ], U32) for g in range(PAGES)]
@@ -215,11 +224,11 @@ def tile_attend_pkv4_soft_kb_gate_kernel(tc, qT, k_words, k_scales, v_words, v_s
         turned_banks = {}
 
         def scale_probs(g):
-            nc.vector.tensor_tensor(scaled[g][:], vs_pool[:].indirect(page_offsets(g)), probs[g][:], ALU.mult)
+            nc.vector.tensor_tensor(scaled[g], vs_pool[:].indirect(page_offsets(g)), probs[g][:], ALU.mult)
 
         def weigh(g):
-            source = scaled[g][:].rearrange("p (s u e) -> p u s e", u=HALVES, e=HALVES)
-            if g == last:
+            source = scaled[g].rearrange("p (s u e) -> p u s e", u=HALVES, e=HALVES)
+            if g == final:
                 nc.vector.tensor_scalar(dealt[g][:], source, rescale[:, g : g + 1], None, ALU.mult)
             else:
                 nc.scalar.activation(dealt[g][:], source, ACT.Copy, scale=rescale[:, g : g + 1])
@@ -243,32 +252,32 @@ def tile_attend_pkv4_soft_kb_gate_kernel(tc, qT, k_words, k_scales, v_words, v_s
         scale_probs(0)
         nc.vector.tensor_reduce(neg_max[:], neg_page_max[:], AXIS_X, ALU.min)
         nc.scalar.activation(rescale[:], neg_page_max[:], ACT.Exp, bias=neg_max[:], scale=-1.0)
-        for g in range(1, PAGES):
+        for g in order[1:]:
             scale_probs(g)
-        for g in range(last):
+        for g in order[:-1]:
             weigh(g)
-        rescaled_sum = sbuf("rescaled_sum", [P, PAGES], F32)
+        rescaled_sum = sbuf("rescaled_sum", [P, PAGES], F32, "probs_then_sum")
         total = sbuf("total", [P, 1], F32)
         inv_total = sbuf("inv_total", [P, 1], F32)
         nc.vector.scalar_tensor_tensor(rescaled_sum[:], page_sum[:], 1.0, rescale[:], ALU.mult, ALU.mult, accum_out=total[:])
-        weigh(last)
-        for g in range(PAGES):
+        weigh(final)
+        for g in order:
             empty_bank(g)
         v_codes = sbuf("v_codes", [P, PAGES * DV], U32, "scaled_then_v")
         nc.vector.tensor_copy(v_codes[:], v_pool[:].indirect(v_offsets[:]))
         nc.vector.reciprocal(inv_total[:], total[:])
-        for g in range(PAGES):
+        for g in order:
             quantise(g)
-        y_bank = bank("y_bank", [P, DV], "bank%d" % (last - 1))
-        for g in range(PAGES):
+        y_bank = bank("y_bank", [P, DV], "bank%d" % order[-2])
+        for g in order:
             nc.tensor.matmul_mx(
                 out=y_bank[:],
                 lhsT=w_codes[g][:].bitcast(FP8X4),
                 lhsT_scale=w_scales[g][:],
                 rhs=v_codes[:, g * DV : (g + 1) * DV].bitcast(FP8X4),
                 rhs_scale=v_plane[:, g * DV : (g + 1) * DV],
-                start=(g == 0),
-                stop=(g == last),
+                start=(g == order[0]),
+                stop=(g == final),
             )
 
         result = sbuf("result", [P, DV], F32)

@@ -51,6 +51,7 @@ def tile_attend_pkv4_soft_kb_gate_kernel(tc, qT, k_words, k_scales, v_words, v_s
         v_offsets = keep.tile([P, PAGES * DV // LIST_ROWS], U16, name="v_offsets")
         cols = PAGE // LIST_ROWS
         last = PAGES - 1
+        BLOCKS = QUADRANTS * SCALE_ROWS
 
         def page_offsets(g):
             return offsets[:, g * cols : (g + 1) * cols]
@@ -104,7 +105,7 @@ def tile_attend_pkv4_soft_kb_gate_kernel(tc, qT, k_words, k_scales, v_words, v_s
                 ACT.Copy,
             )
 
-        q_grouped = [sbuf("q_grouped%d" % o, [P, NQ, PACK], BF16, "q_then_pairs" if o == 0 else None) for o in range(D_PASSES)]
+        q_grouped = [sbuf("q_grouped%d" % o, [P, NQ, PACK], BF16, "q_then_parted%d" % o) for o in range(D_PASSES)]
         q_codes = [sbuf("q_codes%d" % o, [P, NQ], U32) for o in range(D_PASSES)]
         q_scales = [sbuf("q_scales%d" % o, [P, NQ], U8) for o in range(D_PASSES)]
         for o in reversed(range(D_PASSES)):
@@ -122,13 +123,12 @@ def tile_attend_pkv4_soft_kb_gate_kernel(tc, qT, k_words, k_scales, v_words, v_s
         ks_rows = sbuf("ks_rows", [P, SLOTS], U8)
         nc.vector.tensor_copy(ks_rows[:], ks_pool[:].indirect(offsets[:]))
         for o in reversed(range(D_PASSES)):
-            for quad in range(QUADRANTS):
-                target = k_planes[quadrant(quad, SCALE_ROWS), o * SLOTS : (o + 1) * SLOTS].bitcast(I32)
-                first = SCALE_ROWS * (QUADRANTS * o + quad)
-                if first == QUADRANT * quad:
-                    nc.vector.tensor_copy(target, ks_rows[quadrant(quad, SCALE_ROWS), :].bitcast(I32))
-                else:
-                    nc.sync.dma_start(target, ks_rows[first : first + SCALE_ROWS, :].bitcast(I32))
+            for row in range(SCALE_ROWS):
+                first = BLOCKS * o + row
+                nc.sync.dma_start(
+                    k_planes[row:P:QUADRANT, o * SLOTS : (o + 1) * SLOTS].bitcast(I32),
+                    ks_rows[first : BLOCKS * (o + 1) : SCALE_ROWS, :].bitcast(I32),
+                )
 
         nc.sync.dma_start(vs_pool[:], vs)
         nc.sync.dma_start(
@@ -143,8 +143,8 @@ def tile_attend_pkv4_soft_kb_gate_kernel(tc, qT, k_words, k_scales, v_words, v_s
                 vsc_rows[SCALE_ROWS * quad : SCALE_ROWS * (quad + 1), :].bitcast(I32),
             )
 
-        k_pairs = [sbuf("k_pairs%d" % g, [P, PAGE], U32, "q_then_pairs" if g == last else None) for g in range(PAGES)]
-        k_parted = [sbuf("k_parted%d" % g, [P, D_PASSES, FP4_WORD_BYTES * PAGE], U8) for g in range(PAGES)]
+        k_pairs = [sbuf("k_pairs%d" % g, [P, PAGE], U32, "pairs%d" % (1 if g == last else g)) for g in range(PAGES)]
+        k_parted = [sbuf("k_parted%d" % g, [P, D_PASSES, FP4_WORD_BYTES * PAGE], U8, {1: "q_then_parted1", 2: "q_then_parted0"}.get(g)) for g in range(PAGES)]
 
         def gather_keys(g):
             nc.vector.tensor_copy(k_pairs[g][:], k_pool[:].indirect(page_offsets(g)))

@@ -59,13 +59,23 @@ def tile_attend_pkv4_soft_kb_gate_kernel(tc, qT, k_words, k_scales, v_words, v_s
         half_window = TOKENS // 2
         ks_pool = late.tile([P, TOKENS], U8, name="ks_pool", offset=half_window)
         v_pool = late.tile([P, POOL_PAGES * DV], U32, name="v_pool", offset=0)
-        vs_pool = late.tile([P, TOKENS], F32, name="vs_pool", offset=TOKENS)
+        vs_offset = TOKENS + DV * 4
+        vs_pool = late.tile([P, TOKENS], F32, name="vs_pool", offset=vs_offset)
+
+        og_sb = late.tile([P, DV], F32, name="og_sb", offset=TOKENS)
+
+        half = PAGE * 2
+        base = vs_offset + TOKENS * 4
+        parted_shape = [P, D_PASSES, FP4_WORD_BYTES * PAGE]
+        second_parted = late.tile(parted_shape, U8, name="k_parted1", offset=base, align_bytes=64)
+        biases = late.tile([P, SLOTS], F32, name="biases", offset=base + 2 * half)
+        third_parted = late.tile(parted_shape, U8, name="k_parted2", offset=base + 10 * half, align_bytes=64)
+        last_pairs = late.tile([P, PAGE], U32, name="k_pairs3", offset=base + 12 * half)
+        q_raw = [late.tile([P, PACK, NQ], F32, name="q_raw%d" % o, offset=base + (1 if o else 11) * half) for o in range(D_PASSES)]
 
         k_pool = sbuf("k_pool", [P, TOKENS], U32)
-        q_raw = sbuf("q_raw", [P, D_PASSES, PACK, NQ], F32, "q_then_kb")
         kb_columns = sbuf("kb_columns", [P, TOKENS // P], F32)
         vsc_pool = sbuf("vsc_pool", [P, POOL_PAGES * DV], U8)
-        og_sb = sbuf("og_sb", [P, DV], F32)
         nc.vector.memset(vsc_pool[:].bitcast(I32), 0)
         nc.sync.dma_start(ks_pool[quadrant(0), :].bitcast(I32), k_scales.bitcast(I32).rearrange("o f t -> (o f) t"))
         nc.sync.dma_start(offsets[:], offs)
@@ -76,11 +86,11 @@ def tile_attend_pkv4_soft_kb_gate_kernel(tc, qT, k_words, k_scales, v_words, v_s
             v_scales.bitcast(I32).rearrange("u f e -> f u e"),
         )
         nc.sync.dma_start(k_pool[:].bitcast(I32), k_words[0].rearrange("p t b -> p (t b)").bitcast(I32))
-        nc.sync.dma_start(
-            q_raw[:].rearrange("p o j w -> p o (j w)"),
-            qT[0].rearrange("(o p j) w -> p o (j w)", o=D_PASSES, j=PACK),
-        )
-        nc.sync.dma_start(og_sb[:], og[0])
+        for o in reversed(range(D_PASSES)):
+            nc.sync.dma_start(
+                q_raw[o][:].rearrange("p j w -> p (j w)"),
+                qT[0].rearrange("(o p j) w -> o p (j w)", o=D_PASSES, j=PACK)[o],
+            )
 
         k_planes = sbuf("k_planes", [P, D_PASSES * SLOTS], U8)
         v_plane = sbuf("v_plane", [P, PAGES * DV], U8)
@@ -105,20 +115,14 @@ def tile_attend_pkv4_soft_kb_gate_kernel(tc, qT, k_words, k_scales, v_words, v_s
                 ACT.Copy,
             )
 
-        q_grouped = [sbuf("q_grouped%d" % o, [P, NQ, PACK], BF16, "q_then_parted%d" % o) for o in range(D_PASSES)]
+        q_grouped = [sbuf("q_grouped%d" % o, [P, NQ, PACK], BF16) for o in range(D_PASSES)]
         q_codes = [sbuf("q_codes%d" % o, [P, NQ], U32) for o in range(D_PASSES)]
         q_scales = [sbuf("q_scales%d" % o, [P, NQ], U8) for o in range(D_PASSES)]
         for o in reversed(range(D_PASSES)):
-            nc.scalar.copy(q_grouped[o][:], q_raw[:, o].rearrange("p j w -> p w j"))
+            nc.scalar.copy(q_grouped[o][:], q_raw[o][:].rearrange("p j w -> p w j"))
 
-        biases = sbuf("biases", [P, SLOTS], F32, "q_then_kb")
         for g in range(PAGES):
             nc.scalar.activation(biases[:, g * PAGE : (g + 1) * PAGE], kb_pool[:].indirect(page_offsets(g)), ACT.Copy)
-
-        half_tanh = sbuf("half_tanh", [P, DV], F32)
-        gate = sbuf("gate", [P, DV], F32)
-        nc.scalar.activation(half_tanh[:], og_sb[:], ACT.Tanh, scale=0.5)
-        nc.scalar.activation(gate[:], half_tanh[:], ACT.Copy, scale=0.5, bias=0.5)
 
         ks_rows = sbuf("ks_rows", [P, SLOTS], U8)
         nc.vector.tensor_copy(ks_rows[:], ks_pool[:].indirect(offsets[:]))
@@ -142,9 +146,10 @@ def tile_attend_pkv4_soft_kb_gate_kernel(tc, qT, k_words, k_scales, v_words, v_s
                 v_plane[quadrant(quad, SCALE_ROWS), :].bitcast(I32),
                 vsc_rows[SCALE_ROWS * quad : SCALE_ROWS * (quad + 1), :].bitcast(I32),
             )
+        nc.sync.dma_start(og_sb[:], og[0])
 
-        k_pairs = [sbuf("k_pairs%d" % g, [P, PAGE], U32, "pairs%d" % (1 if g == last else g)) for g in range(PAGES)]
-        k_parted = [sbuf("k_parted%d" % g, [P, D_PASSES, FP4_WORD_BYTES * PAGE], U8, {1: "q_then_parted1", 2: "q_then_parted0"}.get(g)) for g in range(PAGES)]
+        k_pairs = [sbuf("k_pairs%d" % g, [P, PAGE], U32) for g in range(last)] + [last_pairs]
+        k_parted = [sbuf("k_parted0", parted_shape, U8), second_parted, third_parted, sbuf("k_parted3", parted_shape, U8)]
 
         def gather_keys(g):
             nc.vector.tensor_copy(k_pairs[g][:], k_pool[:].indirect(page_offsets(g)))
@@ -215,7 +220,7 @@ def tile_attend_pkv4_soft_kb_gate_kernel(tc, qT, k_words, k_scales, v_words, v_s
         scaled_early = sbuf("scaled_early", [P, PAGES - 1, PAGE], F32, "raw_then_scaled")
         scaled = {g: scaled_early[:, place] for place, g in enumerate(order[:-1])}
         scaled[final] = sbuf("scaled_final", [P, PAGE], F32, "scaled_then_v")[:]
-        dealt = [sbuf("dealt%d" % g, [P, HALVES, P, HALVES], BF16) for g in range(PAGES)]
+        dealt = [sbuf("dealt%d" % g, [P, HALVES, P, HALVES], BF16, "dealt_then_gate" if g == final else None) for g in range(PAGES)]
         weights = [sbuf("weights%d" % g, [P, NQ, PACK], BF16) for g in range(PAGES)]
         w_codes = [sbuf("w_codes%d" % g, [P, NQ], U32) for g in range(PAGES)]
         w_scales = [sbuf("w_scales%d" % g, [P, NQ], U8) for g in range(PAGES)]
@@ -263,6 +268,10 @@ def tile_attend_pkv4_soft_kb_gate_kernel(tc, qT, k_words, k_scales, v_words, v_s
         weigh(final)
         for g in order:
             empty_bank(g)
+        half_tanh = sbuf("half_tanh", [P, DV], F32, "dealt_then_gate")
+        gate = sbuf("gate", [P, DV], F32)
+        nc.scalar.activation(half_tanh[:], og_sb[:], ACT.Tanh, scale=0.5)
+        nc.scalar.activation(gate[:], half_tanh[:], ACT.Copy, scale=0.5, bias=0.5)
         v_codes = sbuf("v_codes", [P, PAGES * DV], U32, "scaled_then_v")
         nc.vector.tensor_copy(v_codes[:], v_pool[:].indirect(v_offsets[:]))
         nc.vector.reciprocal(inv_total[:], total[:])

@@ -56,13 +56,12 @@ def tile_attend_pkv4_soft_kb_gate_kernel(tc, qT, k_words, k_scales, v_words, v_s
         def page_offsets(g):
             return offsets[:, g * cols : (g + 1) * cols]
 
-        half_window = TOKENS // 2
-        ks_pool = late.tile([P, TOKENS], U8, name="ks_pool", offset=half_window)
+        v_bytes = POOL_PAGES * DV * 4
+        vs_offset = v_bytes + PAGES * DV
         v_pool = late.tile([P, POOL_PAGES * DV], U32, name="v_pool", offset=0)
-        vs_offset = TOKENS + DV * 4
+        vsc_pool = late.tile([P, POOL_PAGES * DV], U8, name="vsc_pool", offset=v_bytes - 64)
+        v_plane = late.tile([P, PAGES * DV], U8, name="v_plane", offset=v_bytes, align_bytes=64)
         vs_pool = late.tile([P, TOKENS], F32, name="vs_pool", offset=vs_offset)
-
-        og_sb = late.tile([P, DV], F32, name="og_sb", offset=TOKENS)
 
         half = PAGE * 2
         base = vs_offset + TOKENS * 4
@@ -75,7 +74,7 @@ def tile_attend_pkv4_soft_kb_gate_kernel(tc, qT, k_words, k_scales, v_words, v_s
 
         k_pool = sbuf("k_pool", [P, TOKENS], U32)
         kb_columns = sbuf("kb_columns", [P, TOKENS // P], F32)
-        vsc_pool = sbuf("vsc_pool", [P, POOL_PAGES * DV], U8)
+        ks_pool = sbuf("ks_pool", [P, TOKENS], U8, "ks_then_planes")
         nc.vector.memset(vsc_pool[:].bitcast(I32), 0)
         nc.sync.dma_start(ks_pool[quadrant(0), :].bitcast(I32), k_scales.bitcast(I32).rearrange("o f t -> (o f) t"))
         nc.sync.dma_start(offsets[:], offs)
@@ -92,12 +91,8 @@ def tile_attend_pkv4_soft_kb_gate_kernel(tc, qT, k_words, k_scales, v_words, v_s
                 qT[0].rearrange("(o p j) w -> o p (j w)", o=D_PASSES, j=PACK)[o],
             )
 
-        k_planes = sbuf("k_planes", [P, D_PASSES * SLOTS], U8)
-        v_plane = sbuf("v_plane", [P, PAGES * DV], U8)
         nc.vector.memset(ks_pool[quadrant(1), :].bitcast(I32), 0)
         nc.vector.memset(ks_pool[quadrant(2, 2 * QUADRANT), :].bitcast(I32), 0)
-        nc.vector.memset(k_planes[:].bitcast(I32), 0)
-        nc.vector.memset(v_plane[:].bitcast(I32), 0)
 
         identity = sbuf("identity", [P, P], F32)
         make_identity(nc, identity[:])
@@ -124,8 +119,11 @@ def tile_attend_pkv4_soft_kb_gate_kernel(tc, qT, k_words, k_scales, v_words, v_s
         for g in range(PAGES):
             nc.scalar.activation(biases[:, g * PAGE : (g + 1) * PAGE], kb_pool[:].indirect(page_offsets(g)), ACT.Copy)
 
-        ks_rows = sbuf("ks_rows", [P, SLOTS], U8)
+        ks_rows = sbuf("ks_rows", [P, SLOTS], U8, "rows_then_og")
         nc.vector.tensor_copy(ks_rows[:], ks_pool[:].indirect(offsets[:]))
+        vsc_rows = sbuf("vsc_rows", [P, PAGES * DV], U8)
+        nc.vector.tensor_copy(vsc_rows[:], vsc_pool[:].indirect(v_offsets[:]))
+        k_planes = sbuf("k_planes", [P, D_PASSES * SLOTS], U8, "ks_then_planes")
         for o in reversed(range(D_PASSES)):
             for row in range(SCALE_ROWS):
                 first = BLOCKS * o + row
@@ -139,13 +137,12 @@ def tile_attend_pkv4_soft_kb_gate_kernel(tc, qT, k_words, k_scales, v_words, v_s
             v_pool[:].bitcast(I32).rearrange("p (u e) -> p u e", u=POOL_PAGES),
             v_words.rearrange("u p e r -> p u (e r)").bitcast(I32),
         )
-        vsc_rows = sbuf("vsc_rows", [P, PAGES * DV], U8)
-        nc.vector.tensor_copy(vsc_rows[:], vsc_pool[:].indirect(v_offsets[:]))
         for quad in range(QUADRANTS):
             nc.sync.dma_start(
                 v_plane[quadrant(quad, SCALE_ROWS), :].bitcast(I32),
                 vsc_rows[SCALE_ROWS * quad : SCALE_ROWS * (quad + 1), :].bitcast(I32),
             )
+        og_sb = sbuf("og_sb", [P, DV], F32, "rows_then_og")
         nc.sync.dma_start(og_sb[:], og[0])
 
         k_pairs = [sbuf("k_pairs%d" % g, [P, PAGE], U32) for g in range(last)] + [last_pairs]

@@ -66,9 +66,9 @@ def tile_attend_pkv4_soft_kb_gate_kernel(tc, qT, k_words, k_scales, v_words, v_s
         half = PAGE * 2
         base = vs_offset + TOKENS * 4
         parted_shape = [P, D_PASSES, FP4_WORD_BYTES * PAGE]
-        second_parted = late.tile(parted_shape, U8, name="k_parted1", offset=base, align_bytes=64)
+        third_pairs = late.tile([P, PAGE], U32, name="k_pairs2", offset=base)
         biases = late.tile([P, SLOTS], F32, name="biases", offset=base + 2 * half)
-        third_parted = late.tile(parted_shape, U8, name="k_parted2", offset=base + 10 * half, align_bytes=64)
+        second_parted = late.tile(parted_shape, U8, name="k_parted1", offset=base + 10 * half, align_bytes=64)
         last_pairs = late.tile([P, PAGE], U32, name="k_pairs3", offset=base + 12 * half)
         q_raw = [late.tile([P, PACK, NQ], F32, name="q_raw%d" % o, offset=base + (1 if o else 11) * half) for o in range(D_PASSES)]
 
@@ -145,8 +145,8 @@ def tile_attend_pkv4_soft_kb_gate_kernel(tc, qT, k_words, k_scales, v_words, v_s
         og_sb = sbuf("og_sb", [P, DV], F32, "rows_then_og")
         nc.sync.dma_start(og_sb[:], og[0])
 
-        k_pairs = [sbuf("k_pairs%d" % g, [P, PAGE], U32) for g in range(last)] + [last_pairs]
-        k_parted = [sbuf("k_parted0", parted_shape, U8), second_parted, third_parted, sbuf("k_parted3", parted_shape, U8)]
+        k_pairs = [sbuf("k_pairs0", [P, PAGE], U32), sbuf("k_pairs1", [P, PAGE], U32, "pairs_then_parted"), third_pairs, last_pairs]
+        k_parted = [sbuf("k_parted0", parted_shape, U8), second_parted]
 
         def gather_keys(g):
             nc.vector.tensor_copy(k_pairs[g][:], k_pool[:].indirect(page_offsets(g)))
@@ -165,11 +165,12 @@ def tile_attend_pkv4_soft_kb_gate_kernel(tc, qT, k_words, k_scales, v_words, v_s
         gather_keys(0)
         gather_keys(1)
         part_keys(0)
-        gather_keys(2)
         quantise_queries(1)
-        part_keys(1)
+        gather_keys(2)
         quantise_queries(0)
+        part_keys(1)
         gather_keys(last)
+        k_parted.extend([sbuf("k_parted2", parted_shape, U8, "pairs_then_parted"), sbuf("k_parted3", parted_shape, U8)])
         part_keys(last - 1)
         part_keys(last)
 

@@ -174,7 +174,7 @@ def tile_attend_pkv4_soft_kb_gate_kernel(tc, qT, k_words, k_scales, v_words, v_s
         part_keys(last - 1)
         part_keys(last)
 
-        scores = [sbuf("scores%d" % g, [P, PAGE], F32) for g in range(PAGES)]
+        scores = [sbuf("scores%d" % g, [P, PAGE], F32, "scores_vs_then_v" if g == 0 else None) for g in range(PAGES)]
         probs = [sbuf("probs%d" % g, [P, PAGE], F32, "probs_then_sum" if g == last else None) for g in range(PAGES)]
         neg_page_max = sbuf("neg_page_max", [P, PAGES], F32)
         page_sum = sbuf("page_sum", [P, PAGES], F32)
@@ -208,17 +208,17 @@ def tile_attend_pkv4_soft_kb_gate_kernel(tc, qT, k_words, k_scales, v_words, v_s
         nc.gpsimd.tensor_tensor(scores[aside][:], raw_scores[:], biases[:, aside * PAGE : (aside + 1) * PAGE], ALU.add)
         order = [g for g in range(PAGES) if g != aside] + [aside]
         add_bias(order[0])
-        for earlier, g in zip(order, order[1:-1]):
-            add_bias(g)
-            page_softmax(earlier)
-        for g in order[-2:]:
+        add_bias(order[1])
+        page_softmax(order[0])
+        listed_vs = sbuf("listed_vs", [P, PAGE], F32, "scores_vs_then_v")
+        nc.scalar.activation(listed_vs[:], vs_pool[:].indirect(page_offsets(aside)), ACT.Copy)
+        add_bias(order[2])
+        for g in order[1:]:
             page_softmax(g)
-        final = order[-1]
 
         scaled_early = sbuf("scaled_early", [P, PAGES - 1, PAGE], F32, "raw_then_scaled")
         scaled = {g: scaled_early[:, place] for place, g in enumerate(order[:-1])}
-        scaled[final] = sbuf("scaled_final", [P, PAGE], F32, "scaled_then_v")[:]
-        dealt = [sbuf("dealt%d" % g, [P, HALVES, P, HALVES], BF16, "dealt_then_gate" if g == final else None) for g in range(PAGES)]
+        dealt = [sbuf("dealt%d" % g, [P, HALVES, P, HALVES], BF16, "dealt_then_gate" if g == last else None) for g in range(PAGES)]
         weights = [sbuf("weights%d" % g, [P, NQ, PACK], BF16) for g in range(PAGES)]
         w_codes = [sbuf("w_codes%d" % g, [P, NQ], U32) for g in range(PAGES)]
         w_scales = [sbuf("w_scales%d" % g, [P, NQ], U8) for g in range(PAGES)]
@@ -229,12 +229,19 @@ def tile_attend_pkv4_soft_kb_gate_kernel(tc, qT, k_words, k_scales, v_words, v_s
         def scale_probs(g):
             nc.vector.tensor_tensor(scaled[g], vs_pool[:].indirect(page_offsets(g)), probs[g][:], ALU.mult)
 
+        def deal(values):
+            return values.rearrange("p (s u e) -> p u s e", u=HALVES, e=HALVES)
+
         def weigh(g):
-            source = scaled[g].rearrange("p (s u e) -> p u s e", u=HALVES, e=HALVES)
-            if g == final:
-                nc.vector.tensor_scalar(dealt[g][:], source, rescale[:, g : g + 1], None, ALU.mult)
+            if g == aside:
+                for u in range(HALVES):
+                    nc.vector.scalar_tensor_tensor(
+                        dealt[g][:, u], deal(probs[g][:])[:, u], rescale[:, g : g + 1], deal(listed_vs[:])[:, u], ALU.mult, ALU.mult
+                    )
+            elif g == last:
+                nc.vector.tensor_scalar(dealt[g][:], deal(scaled[g]), rescale[:, g : g + 1], None, ALU.mult)
             else:
-                nc.scalar.activation(dealt[g][:], source, ACT.Copy, scale=rescale[:, g : g + 1])
+                nc.scalar.activation(dealt[g][:], deal(scaled[g]), ACT.Copy, scale=rescale[:, g : g + 1])
             turned = bank("turned%d" % g, [P, HALVES, NQ], "bank%d" % g)
             words = dealt[g][:].rearrange("p u s e -> p (u s e)").bitcast(F32)
             for u in range(HALVES):
@@ -255,36 +262,37 @@ def tile_attend_pkv4_soft_kb_gate_kernel(tc, qT, k_words, k_scales, v_words, v_s
         scale_probs(0)
         nc.vector.tensor_reduce(neg_max[:], neg_page_max[:], AXIS_X, ALU.min)
         nc.scalar.activation(rescale[:], neg_page_max[:], ACT.Exp, bias=neg_max[:], scale=-1.0)
-        for g in order[1:]:
+        for g in order[1:-1]:
             scale_probs(g)
-        for g in order[:-1]:
+        for g in order[:-2]:
             weigh(g)
         rescaled_sum = sbuf("rescaled_sum", [P, PAGES], F32, "probs_then_sum")
         total = sbuf("total", [P, 1], F32)
         inv_total = sbuf("inv_total", [P, 1], F32)
         nc.vector.scalar_tensor_tensor(rescaled_sum[:], page_sum[:], 1.0, rescale[:], ALU.mult, ALU.mult, accum_out=total[:])
-        weigh(final)
-        for g in order:
+        weigh(aside)
+        weigh(last)
+        for g in range(PAGES):
             empty_bank(g)
         half_tanh = sbuf("half_tanh", [P, DV], F32, "dealt_then_gate")
         gate = sbuf("gate", [P, DV], F32)
         nc.scalar.activation(half_tanh[:], og_sb[:], ACT.Tanh, scale=0.5)
         nc.scalar.activation(gate[:], half_tanh[:], ACT.Copy, scale=0.5, bias=0.5)
-        v_codes = sbuf("v_codes", [P, PAGES * DV], U32, "scaled_then_v")
+        v_codes = sbuf("v_codes", [P, PAGES * DV], U32, "scores_vs_then_v")
         nc.vector.tensor_copy(v_codes[:], v_pool[:].indirect(v_offsets[:]))
         nc.vector.reciprocal(inv_total[:], total[:])
-        for g in order:
+        for g in range(PAGES):
             quantise(g)
-        y_bank = bank("y_bank", [P, DV], "bank%d" % order[-2])
-        for g in order:
+        y_bank = bank("y_bank", [P, DV], "bank%d" % aside)
+        for g in range(PAGES):
             nc.tensor.matmul_mx(
                 out=y_bank[:],
                 lhsT=w_codes[g][:].bitcast(FP8X4),
                 lhsT_scale=w_scales[g][:],
                 rhs=v_codes[:, g * DV : (g + 1) * DV].bitcast(FP8X4),
                 rhs_scale=v_plane[:, g * DV : (g + 1) * DV],
-                start=(g == order[0]),
-                stop=(g == final),
+                start=(g == 0),
+                stop=(g == last),
             )
 
         result = sbuf("result", [P, DV], F32)

from contextlib import ExitStack

import concourse.mybir as mybir
from concourse.masks import make_identity

F32 = mybir.dt.float32
BF16 = mybir.dt.bfloat16
I32 = mybir.dt.int32
U32 = mybir.dt.uint32
U16 = mybir.dt.uint16
U8 = mybir.dt.uint8
FP8X4 = mybir.dt.float8_e4m3fn_x4
FP4X4 = mybir.dt.float4_e2m1fn_x4
ALU = mybir.AluOpType
ACT = mybir.ActivationFunctionType
AXIS_X = mybir.AxisListType.X

P = 128
PACK = 4
SLOTS, TOKENS, D, DV, NQ = 2048, 4096, 1024, 128, 128
PAGE = 512
PAGES = SLOTS // PAGE
POOL_PAGES = TOKENS // PAGE
D_PASSES = D // (P * PACK)
QUADRANTS, QUADRANT = 4, 32
SCALE_ROWS = 4
LIST_ROWS = 16
HALVES = 2
FP4_WORD_BYTES = 2

FLOPS = 2 * NQ * SLOTS * (D + DV)


def tile_attend_pkv4_soft_kb_gate_kernel(tc, qT, k_words, k_scales, v_words, v_scales, vs, kb, og, offs, voffs, out):
    nc = tc.nc
    with ExitStack() as ctx:
        keep = ctx.enter_context(tc.tile_pool(name="keep", bufs=1))
        late = ctx.enter_context(tc.tile_pool(name="late", bufs=1))
        psum = ctx.enter_context(tc.psum_pool(name="psum", bufs=1))

        def sbuf(name, shape, dtype, tag=None):
            return keep.tile(shape, dtype, name=name, tag=tag or name, align_bytes=64)

        def bank(name, shape, tag):
            return psum.tile(shape, F32, name=name, tag=tag)

        def quadrant(quad, rows=QUADRANT):
            return slice(QUADRANT * quad, QUADRANT * quad + rows)

        offsets = keep.tile([P, SLOTS // LIST_ROWS], U16, name="offsets")
        v_offsets = keep.tile([P, PAGES * DV // LIST_ROWS], U16, name="v_offsets")
        cols = PAGE // LIST_ROWS
        last = PAGES - 1
        BLOCKS = QUADRANTS * SCALE_ROWS

        def page_offsets(g):
            return offsets[:, g * cols : (g + 1) * cols]

        v_bytes = POOL_PAGES * DV * 4
        vs_offset = v_bytes + PAGES * DV
        v_pool = late.tile([P, POOL_PAGES * DV], U32, name="v_pool", offset=0)
        vsc_pool = late.tile([P, POOL_PAGES * DV], U8, name="vsc_pool", offset=v_bytes - 64)
        v_plane = late.tile([P, PAGES * DV], U8, name="v_plane", offset=v_bytes, align_bytes=64)
        vs_pool = late.tile([P, TOKENS], F32, name="vs_pool", offset=vs_offset)

        half = PAGE * 2
        base = vs_offset + TOKENS * 4
        parted_shape = [P, D_PASSES, FP4_WORD_BYTES * PAGE]
        third_pairs = late.tile([P, PAGE], U32, name="k_pairs2", offset=base)
        biases = late.tile([P, SLOTS], F32, name="biases", offset=base + 2 * half)
        second_parted = late.tile(parted_shape, U8, name="k_parted1", offset=base + 10 * half, align_bytes=64)
        last_pairs = late.tile([P, PAGE], U32, name="k_pairs3", offset=base + 12 * half)
        q_raw = [late.tile([P, PACK, NQ], F32, name="q_raw%d" % o, offset=base + (1 if o else 11) * half) for o in range(D_PASSES)]

        k_pool = sbuf("k_pool", [P, TOKENS], U32)
        kb_columns = sbuf("kb_columns", [P, TOKENS // P], F32)
        ks_pool = sbuf("ks_pool", [P, TOKENS], U8, "ks_then_planes")
        nc.vector.memset(vsc_pool[:].bitcast(I32), 0)
        nc.sync.dma_start(ks_pool[quadrant(0), :].bitcast(I32), k_scales.bitcast(I32).rearrange("o f t -> (o f) t"))
        nc.sync.dma_start(offsets[:], offs)
        nc.sync.dma_start(kb_columns[:], kb[0].rearrange("(p c) -> p c", p=P))
        nc.sync.dma_start(v_offsets[:], voffs)
        nc.sync.dma_start(
            vsc_pool[: QUADRANTS * SCALE_ROWS, :].bitcast(I32).rearrange("f (u e) -> f u e", u=POOL_PAGES),
            v_scales.bitcast(I32).rearrange("u f e -> f u e"),
        )
        nc.sync.dma_start(k_pool[:].bitcast(I32), k_words[0].rearrange("p t b -> p (t b)").bitcast(I32))
        for o in reversed(range(D_PASSES)):
            nc.sync.dma_start(
                q_raw[o][:].rearrange("p j w -> p (j w)"),
                qT[0].rearrange("(o p j) w -> o p (j w)", o=D_PASSES, j=PACK)[o],
            )

        nc.vector.memset(ks_pool[quadrant(1), :].bitcast(I32), 0)
        nc.vector.memset(ks_pool[quadrant(2, 2 * QUADRANT), :].bitcast(I32), 0)

        identity = sbuf("identity", [P, P], F32)
        make_identity(nc, identity[:])

        kb_pool = sbuf("kb_pool", [P, TOKENS], F32)
        per_bank = PAGE // P
        for b in range(TOKENS // PAGE):
            spread = bank("spread%d" % b, [P, per_bank, P], "spread_bank%d" % (b % PAGES))
            for c in range(per_bank):
                column = b * per_bank + c
                nc.tensor.transpose(spread[:, c, :], kb_columns[:, column : column + 1].to_broadcast([P, P]), identity[:])
            nc.scalar.activation(
                kb_pool[:].rearrange("q (p b c) -> q b p c", p=P, c=per_bank)[:, b],
                spread[:].rearrange("q c p -> q p c"),
                ACT.Copy,
            )

        q_grouped = [sbuf("q_grouped%d" % o, [P, NQ, PACK], BF16) for o in range(D_PASSES)]
        q_codes = [sbuf("q_codes%d" % o, [P, NQ], U32) for o in range(D_PASSES)]
        q_scales = [sbuf("q_scales%d" % o, [P, NQ], U8) for o in range(D_PASSES)]
        for o in reversed(range(D_PASSES)):
            nc.scalar.copy(q_grouped[o][:], q_raw[o][:].rearrange("p j w -> p w j"))

        for g in range(PAGES):
            nc.scalar.activation(biases[:, g * PAGE : (g + 1) * PAGE], kb_pool[:].indirect(page_offsets(g)), ACT.Copy)

        ks_rows = sbuf("ks_rows", [P, SLOTS], U8, "rows_then_og")
        nc.vector.tensor_copy(ks_rows[:], ks_pool[:].indirect(offsets[:]))
        vsc_rows = sbuf("vsc_rows", [P, PAGES * DV], U8)
        nc.vector.tensor_copy(vsc_rows[:], vsc_pool[:].indirect(v_offsets[:]))
        k_planes = sbuf("k_planes", [P, D_PASSES * SLOTS], U8, "ks_then_planes")
        for o in reversed(range(D_PASSES)):
            for row in range(SCALE_ROWS):
                first = BLOCKS * o + row
                nc.sync.dma_start(
                    k_planes[row:P:QUADRANT, o * SLOTS : (o + 1) * SLOTS].bitcast(I32),
                    ks_rows[first : BLOCKS * (o + 1) : SCALE_ROWS, :].bitcast(I32),
                )

        nc.sync.dma_start(vs_pool[:], vs)
        nc.sync.dma_start(
            v_pool[:].bitcast(I32).rearrange("p (u e) -> p u e", u=POOL_PAGES),
            v_words.rearrange("u p e r -> p u (e r)").bitcast(I32),
        )
        for quad in range(QUADRANTS):
            nc.sync.dma_start(
                v_plane[quadrant(quad, SCALE_ROWS), :].bitcast(I32),
                vsc_rows[SCALE_ROWS * quad : SCALE_ROWS * (quad + 1), :].bitcast(I32),
            )
        og_sb = sbuf("og_sb", [P, DV], F32, "rows_then_og")
        nc.sync.dma_start(og_sb[:], og[0])

        k_pairs = [sbuf("k_pairs0", [P, PAGE], U32), sbuf("k_pairs1", [P, PAGE], U32, "pairs_then_parted"), third_pairs, last_pairs]
        k_parted = [sbuf("k_parted0", parted_shape, U8), second_parted]

        def gather_keys(g):
            nc.vector.tensor_copy(k_pairs[g][:], k_pool[:].indirect(page_offsets(g)))

        def part_keys(g):
            nc.vector.tensor_copy(
                k_parted[g][:].bitcast(U16),
                k_pairs[g][:].bitcast(U16).rearrange("p (s o) -> p o s", o=D_PASSES),
            )

        def quantise_queries(o):
            nc.vector.quantize_mx(
                out=q_codes[o][:].bitcast(FP8X4), scales=q_scales[o][:], in_=q_grouped[o][:].rearrange("p w j -> p (w j)")
            )

        gather_keys(0)
        gather_keys(1)
        part_keys(0)
        quantise_queries(1)
        gather_keys(2)
        quantise_queries(0)
        part_keys(1)
        gather_keys(last)
        k_parted.extend([sbuf("k_parted2", parted_shape, U8, "pairs_then_parted"), sbuf("k_parted3", parted_shape, U8)])
        part_keys(last - 1)
        part_keys(last)

        scores = [sbuf("scores%d" % g, [P, PAGE], F32, "scores_vs_then_v" if g == 0 else None) for g in range(PAGES)]
        probs = [sbuf("probs%d" % g, [P, PAGE], F32, "probs_then_sum" if g == last else None) for g in range(PAGES)]
        neg_page_max = sbuf("neg_page_max", [P, PAGES], F32)
        page_sum = sbuf("page_sum", [P, PAGES], F32)
        score_banks = []
        for g in range(PAGES):
            score_bank = bank("score_bank%d" % g, [P, PAGE], "bank%d" % g)
            for o in reversed(range(D_PASSES)):
                nc.tensor.matmul_mx(
                    out=score_bank[:],
                    lhsT=q_codes[o][:].bitcast(FP8X4),
                    lhsT_scale=q_scales[o][:],
                    rhs=k_parted[g][:, o, :].bitcast(FP4X4),
                    rhs_scale=k_planes[:, o * SLOTS + g * PAGE : o * SLOTS + (g + 1) * PAGE],
                    start=(o == D_PASSES - 1),
                    stop=(o == 0),
                )
            score_banks.append(score_bank)

        def add_bias(g):
            nc.vector.tensor_tensor(scores[g][:], score_banks[g][:], biases[:, g * PAGE : (g + 1) * PAGE], ALU.add)

        def page_softmax(g):
            nc.vector.tensor_reduce(neg_page_max[:, g : g + 1], scores[g][:], AXIS_X, ALU.max, negate=True)
            nc.scalar.activation(
                probs[g][:], scores[g][:], ACT.Exp, bias=neg_page_max[:, g : g + 1], accum_out=page_sum[:, g : g + 1]
            )

        aside = last - 1
        raw_scores = sbuf("raw_scores", [P, PAGE], F32, "raw_then_scaled")
        nc.scalar.copy(raw_scores[:], score_banks[aside][:])
        nc.gpsimd.tensor_tensor(scores[aside][:], raw_scores[:], biases[:, aside * PAGE : (aside + 1) * PAGE], ALU.add)
        order = [g for g in range(PAGES) if g != aside] + [aside]
        add_bias(order[0])
        add_bias(order[1])
        page_softmax(order[0])
        listed_vs = sbuf("listed_vs", [P, PAGE], F32, "scores_vs_then_v")
        nc.scalar.activation(listed_vs[:], vs_pool[:].indirect(page_offsets(aside)), ACT.Copy)
        add_bias(order[2])
        for g in order[1:]:
            page_softmax(g)

        scaled_early = sbuf("scaled_early", [P, PAGES - 1, PAGE], F32, "raw_then_scaled")
        scaled = {g: scaled_early[:, place] for place, g in enumerate(order[:-1])}
        dealt = [sbuf("dealt%d" % g, [P, HALVES, P, HALVES], BF16, "dealt_then_gate" if g == last else None) for g in range(PAGES)]
        weights = [sbuf("weights%d" % g, [P, NQ, PACK], BF16) for g in range(PAGES)]
        w_codes = [sbuf("w_codes%d" % g, [P, NQ], U32) for g in range(PAGES)]
        w_scales = [sbuf("w_scales%d" % g, [P, NQ], U8) for g in range(PAGES)]
        neg_max = sbuf("neg_max", [P, 1], F32)
        rescale = sbuf("rescale", [P, PAGES], F32)
        turned_banks = {}

        def scale_probs(g):
            nc.vector.tensor_tensor(scaled[g], vs_pool[:].indirect(page_offsets(g)), probs[g][:], ALU.mult)

        def deal(values):
            return values.rearrange("p (s u e) -> p u s e", u=HALVES, e=HALVES)

        def weigh(g):
            if g == aside:
                for u in range(HALVES):
                    nc.vector.scalar_tensor_tensor(
                        dealt[g][:, u], deal(probs[g][:])[:, u], rescale[:, g : g + 1], deal(listed_vs[:])[:, u], ALU.mult, ALU.mult
                    )
            elif g == last:
                nc.vector.tensor_scalar(dealt[g][:], deal(scaled[g]), rescale[:, g : g + 1], None, ALU.mult)
            else:
                nc.scalar.activation(dealt[g][:], deal(scaled[g]), ACT.Copy, scale=rescale[:, g : g + 1])
            turned = bank("turned%d" % g, [P, HALVES, NQ], "bank%d" % g)
            words = dealt[g][:].rearrange("p u s e -> p (u s e)").bitcast(F32)
            for u in range(HALVES):
                nc.tensor.transpose(turned[:, u, :], words[:, u * P : (u + 1) * P], identity[:])
            turned_banks[g] = turned

        def empty_bank(g):
            nc.scalar.copy(
                weights[g][:].rearrange("p q r -> p (q r)").bitcast(F32).rearrange("p (q u) -> p q u", u=HALVES),
                turned_banks[g][:].rearrange("p u q -> p q u"),
            )

        def quantise(g):
            nc.vector.quantize_mx(
                out=w_codes[g][:].bitcast(FP8X4), scales=w_scales[g][:], in_=weights[g][:].rearrange("p q r -> p (q r)")
            )

        scale_probs(0)
        nc.vector.tensor_reduce(neg_max[:], neg_page_max[:], AXIS_X, ALU.min)
        nc.scalar.activation(rescale[:], neg_page_max[:], ACT.Exp, bias=neg_max[:], scale=-1.0)
        for g in order[1:-1]:
            scale_probs(g)
        for g in order[:-2]:
            weigh(g)
        rescaled_sum = sbuf("rescaled_sum", [P, PAGES], F32, "probs_then_sum")
        total = sbuf("total", [P, 1], F32)
        inv_total = sbuf("inv_total", [P, 1], F32)
        nc.vector.scalar_tensor_tensor(rescaled_sum[:], page_sum[:], 1.0, rescale[:], ALU.mult, ALU.mult, accum_out=total[:])
        weigh(aside)
        weigh(last)
        for g in range(PAGES):
            empty_bank(g)
        half_tanh = sbuf("half_tanh", [P, DV], F32, "dealt_then_gate")
        gate = sbuf("gate", [P, DV], F32)
        nc.scalar.activation(half_tanh[:], og_sb[:], ACT.Tanh, scale=0.5)
        nc.scalar.activation(gate[:], half_tanh[:], ACT.Copy, scale=0.5, bias=0.5)
        v_codes = sbuf("v_codes", [P, PAGES * DV], U32, "scores_vs_then_v")
        nc.vector.tensor_copy(v_codes[:], v_pool[:].indirect(v_offsets[:]))
        nc.vector.reciprocal(inv_total[:], total[:])
        for g in range(PAGES):
            quantise(g)
        y_bank = bank("y_bank", [P, DV], "bank%d" % aside)
        for g in range(PAGES):
            nc.tensor.matmul_mx(
                out=y_bank[:],
                lhsT=w_codes[g][:].bitcast(FP8X4),
                lhsT_scale=w_scales[g][:],
                rhs=v_codes[:, g * DV : (g + 1) * DV].bitcast(FP8X4),
                rhs_scale=v_plane[:, g * DV : (g + 1) * DV],
                start=(g == 0),
                stop=(g == last),
            )

        result = sbuf("result", [P, DV], F32)
        nc.vector.scalar_tensor_tensor(result[:], y_bank[:], inv_total[:], gate[:], ALU.mult, ALU.mult)
        nc.sync.dma_start(out[0], result[:])
